import numpy as np
import ml_dtypes


def mxq(x, axis, fmt="e4m3"):
    dtype, down = {"e4m3": (ml_dtypes.float8_e4m3fn, 7), "e5m2": (ml_dtypes.float8_e5m2, 14)}[fmt]
    v = np.moveaxis(np.asarray(x, np.float32).astype(ml_dtypes.bfloat16).astype(np.float64), axis, -1)
    blocks = v.reshape(v.shape[:-1] + (-1, 32))
    amax = np.abs(blocks).max(-1, keepdims=True)
    byte = np.maximum(np.where(amax > 0, np.frexp(amax)[1] - 1 + 127, 0) - down, 1)
    scale = np.exp2(byte - 127.0)
    codes = (blocks / scale).astype(np.float32).astype(dtype).astype(np.float64)
    return np.moveaxis((codes * scale).reshape(v.shape), -1, axis)


WIDE = False


def mx_kscale(k):
    if not WIDE:
        return np.ones(k)
    levels = np.array([10, -10, 5, -5, 0])
    if k % 512:
        return np.exp2(np.random.permutation(np.resize(levels, k // 32))).repeat(32)
    a = np.empty((k // 512, 16))
    for p in range(k // 512):
        a[p, :8] = np.random.permutation(np.resize(levels, 8))
        for g in range(8):
            far = levels[np.abs(levels - a[p, g]) >= 10]
            a[p, g + 8] = far[np.random.randint(len(far))]
    return np.exp2(a.ravel()).repeat(32)


def f64(x):
    return np.asarray(x).astype(np.float64)


def striped(idx):
    return np.tile(idx.reshape(-1, 16).T, (8, 1)).astype(np.uint16)


def unstriped(offs):
    return offs[:16].T.reshape(-1).astype(np.int64)


def pack_weight(w):
    k, n = w.shape
    w = f64(np.asarray(w, np.float32).astype(ml_dtypes.bfloat16)).reshape(k // 32, 32, n)
    amax = np.abs(w).max(1)
    byte = np.clip(np.where(amax > 0, np.frexp(amax)[1] - 1 + 127 - 7, 1), 1, 254)
    scaled = (w * np.exp2(127.0 - byte)[:, None, :]).reshape(k, n).astype(np.float32)
    words = np.ascontiguousarray(scaled.reshape(k // 512, 128, 4, n).transpose(0, 1, 3, 2)).astype(ml_dtypes.float8_e4m3fn).view(np.uint8)
    return words, np.ascontiguousarray(byte.astype(np.uint8).reshape(k // 512, 16, n))


def unpack_weight(words, scales):
    g, p, n, _ = words.shape
    vals = np.ascontiguousarray(words).view(ml_dtypes.float8_e4m3fn).astype(np.float64) * np.repeat(np.exp2(scales.astype(np.float64) - 127.0), 8, axis=1)[..., None]
    return vals.transpose(0, 1, 3, 2).reshape(g * 512, n)


E2M1 = np.array([0.0, 0.5, 1.0, 1.5, 2.0, 3.0, 4.0, 6.0, -0.0, -0.5, -1.0, -1.5, -2.0, -3.0, -4.0, -6.0])


def pack_fp4(w):
    k, n = w.shape
    w = f64(np.asarray(w, np.float32).astype(ml_dtypes.bfloat16)).reshape(k // 32, 32, n)
    amax = np.abs(w).max(1)
    mant, ex = np.frexp(amax / 6.0)
    byte = np.clip(np.where(amax > 0, np.where(mant > 0.5, ex, ex - 1) + 127, 1), 1, 254)
    scaled = (w * np.exp2(127.0 - byte)[:, None, :]).reshape(k, n).astype(np.float32)
    c = np.ascontiguousarray(scaled.reshape(k // 512, 128, 4, n).transpose(0, 1, 3, 2)).astype(ml_dtypes.float4_e2m1fn).view(np.uint8) & 0xF
    words = (c[..., 0::2] | (c[..., 1::2] << 4)).reshape(k // 512, 128, 2 * n)
    return np.ascontiguousarray(words), np.ascontiguousarray(byte.astype(np.uint8).reshape(k // 512, 16, n))


def unpack_fp4(words, scales):
    g, _, n = scales.shape
    words = np.ascontiguousarray(words).reshape(g, 128, n, 2)
    nib = np.empty((g, 128, n, 4), np.uint8)
    nib[..., 0::2] = words & 0xF
    nib[..., 1::2] = words >> 4
    vals = E2M1[nib] * np.repeat(np.exp2(scales.astype(np.float64) - 127.0), 8, axis=1)[..., None]
    return vals.transpose(0, 1, 3, 2).reshape(g * 512, n)


def planes(y):
    n, m = y.shape
    v = y.astype(np.float32).astype(ml_dtypes.bfloat16).astype(np.float64).reshape(n // 32, 32, m)
    top = np.abs(v).max(1)
    byte = np.clip(np.where(top > 0, np.frexp(top)[1] - 1 + 127 - 7, 1), 1, 254)
    codes = (v * np.exp2(127.0 - byte)[:, None, :]).reshape(n, m).astype(np.float32).astype(ml_dtypes.float8_e4m3fn).view(np.uint8)
    words = codes.reshape(n // 512, 128, 4, m).transpose(0, 1, 3, 2)
    return np.ascontiguousarray(words), np.ascontiguousarray(byte.astype(np.uint8).reshape(n // 512, 16, m))


def sigmoid(v):
    return 1.0 / (1.0 + np.exp(-np.maximum(v, -700.0)))


K, T, S, H = 512, 1024, 512, 512


def setup_inputs():
    n = np.random.standard_normal
    s = mx_kscale(K)[:, None]
    u = mx_kscale(H)
    packed_xT = pack_weight(n((K, T)) * s)
    packed_w2 = pack_fp4(n((H, H)) / np.sqrt(H) / u[:, None])
    return {
        "x_words": packed_xT[0],
        "x_scales": packed_xT[1],
        "w1": (n((K, H)) / np.sqrt(K) / s * u).astype(np.float32),
        "w2_words": packed_w2[0],
        "w2_scales": packed_w2[1],
        "offs": striped(np.random.permutation(T)[:S]),
    }


def reference(x_words, x_scales, w1, w2_words, w2_scales, offs):
    xq = unpack_weight(x_words, x_scales)[:, unstriped(offs)]
    h = mxq(f64(w1), 0, "e4m3").T @ xq
    g = sigmoid(unpack_fp4(w2_words, w2_scales).T @ mxq(h, 0, "e4m3"))
    out_0 = h * g
    return (out_0,) + planes(out_0)

@@ -1,0 +1,150 @@
+from contextlib import ExitStack
+
+import concourse.mybir as mybir
+
+F32 = mybir.dt.float32
+BF16 = mybir.dt.bfloat16
+I32 = mybir.dt.int32
+U32 = mybir.dt.uint32
+U16 = mybir.dt.uint16
+U8 = mybir.dt.uint8
+FP8X4 = mybir.dt.float8_e4m3fn_x4
+FP4X4 = mybir.dt.float4_e2m1fn_x4
+SIGMOID = mybir.ActivationFunctionType.Sigmoid
+MULT = mybir.AluOpType.mult
+
+P = 128
+PACK = 4
+K, T, S, H = 512, 1024, 512, 512
+CHUNK = 128
+CHUNKS = S // CHUNK
+FLOPS = 2 * K * H * S + 2 * H * H * S
+
+
+def tile_picked_zgrn_lin_po_kernel(tc, x_words, x_scales, w1, w2_words, w2_scales, offs, out_0, out_1, out_2):
+    nc = tc.nc
+    with ExitStack() as ctx:
+        keep = ctx.enter_context(tc.tile_pool(name="keep", bufs=1))
+        psum = ctx.enter_context(tc.psum_pool(name="psum", bufs=1))
+
+        warm_in = keep.tile([P, 8], F32, name="warm_in")
+        warm_out = keep.tile([P, 8], F32, name="warm_out")
+        nc.gpsimd.memset(warm_in[:], 0.0)
+        nc.scalar.activation(out=warm_out[:], in_=warm_in[:], func=SIGMOID)
+
+        offsets = keep.tile([P, S // 16], U16, name="offsets")
+        nc.sync.dma_start(offsets[:], offs)
+
+        xs_win = keep.tile([P, T], U8, name="xs_win", align_bytes=64)
+        for q in range(4):
+            nc.sync.dma_start(
+                out=xs_win[32 * q : 32 * q + 32, :].bitcast(I32),
+                in_=x_scales[0, 4 * q : 4 * q + 4, :].bitcast(I32).unsqueeze(0).broadcast_to([8, 4, T // 4]),
+            )
+        w1_rows = w1.rearrange("(p j) c -> p j c", j=PACK)
+        w1_raw = []
+        for h in range(2):
+            raw = keep.tile([P, PACK, H // 2], F32, name="w1_raw%d" % h)
+            nc.sync.dma_start(out=raw[:], in_=w1_rows[:, :, h * (H // 2) : (h + 1) * (H // 2)])
+            w1_raw.append(raw)
+        xw_win = keep.tile([P, T], I32, name="xw_win", align_bytes=64)
+        nc.sync.dma_start(out=xw_win[:], in_=x_words[0].rearrange("p c r -> p (c r)").bitcast(I32))
+
+        w2s_raw = keep.tile([P, H], U8, name="w2s_raw", align_bytes=64)
+        for q in range(4):
+            nc.sync.dma_start(
+                out=w2s_raw[32 * q : 32 * q + 32, :].bitcast(I32),
+                in_=w2_scales[0, 4 * q : 4 * q + 4, :].bitcast(I32).unsqueeze(0).broadcast_to([8, 4, H // 4]),
+            )
+        w2w_raw = keep.tile([P, 2 * H], U8, name="w2w_raw", align_bytes=64)
+        nc.sync.dma_start(out=w2w_raw[:].bitcast(I32), in_=w2_words[0].bitcast(I32))
+
+        xs = keep.tile([P, S], U8, name="xs", align_bytes=64)
+        nc.vector.tensor_copy(xs[:], xs_win[:].indirect(offsets[:]))
+
+        w1_bf = keep.tile([P, H * PACK], BF16, name="w1_bf", align_bytes=64)
+        w1_dealt = w1_bf[:].rearrange("p (t m j) -> p m j t", t=PACK, j=PACK)
+        half = P // 2
+        nc.scalar.copy(out=w1_dealt[:, 0:half], in_=w1_raw[0][:].rearrange("p j (m t) -> p m j t", t=PACK))
+        nc.vector.tensor_copy(out=w1_dealt[:, half:P], in_=w1_raw[1][:].rearrange("p j (m t) -> p m j t", t=PACK))
+        w1q = keep.tile([P, H], U32, name="w1q", align_bytes=64)
+        w1s = keep.tile([P, H], U8, name="w1s", align_bytes=64)
+        nc.vector.quantize_mx(out=w1q[:].bitcast(FP8X4), scales=w1s[:], in_=w1_bf[:])
+
+        oq = keep.tile([P, S], U32, name="oq", align_bytes=64)
+        os_ = keep.tile([P, S], U8, name="os_", align_bytes=64)
+        out_rows = out_0.rearrange("(p t) n -> p t n", t=PACK)
+        out_words = out_1[0].rearrange("p c r -> p (c r)").bitcast(I32)
+
+        xw, hb, zb, h_bf, hq, hs, g, o32, o_bf = {}, {}, {}, {}, {}, {}, {}, {}, {}
+
+        def cols(c):
+            return slice(c * CHUNK, (c + 1) * CHUNK)
+
+        def gather(c):
+            xw[c] = keep.tile([P, CHUNK], U32, name="xw%d" % c, align_bytes=64)
+            nc.vector.tensor_copy(xw[c][:], xw_win[:].bitcast(U32).indirect(offsets[:, c * 8 : (c + 1) * 8]))
+
+        def first(c):
+            hb[c] = psum.tile([P, PACK, CHUNK], F32, name="hb%d" % c)
+            for t in range(PACK):
+                nc.tensor.matmul_mx(out=hb[c][:, t, :], lhsT=w1q[:, t * P : (t + 1) * P].bitcast(FP8X4), lhsT_scale=w1s[:, t * P : (t + 1) * P],
+                                    rhs=xw[c][:].bitcast(FP8X4), rhs_scale=xs[:, cols(c)], start=True, stop=True)
+
+        def round_h(c):
+            h_bf[c] = keep.tile([P, CHUNK, PACK], BF16, name="h_bf%d" % c, align_bytes=64)
+            nc.scalar.copy(out=h_bf[c][:], in_=hb[c][:].rearrange("p t n -> p n t"))
+
+        def quant_h(c):
+            hq[c] = keep.tile([P, CHUNK], U32, name="hq%d" % c, align_bytes=64)
+            hs[c] = keep.tile([P, CHUNK], U8, name="hs%d" % c, align_bytes=64)
+            nc.vector.quantize_mx(out=hq[c][:].bitcast(FP8X4), scales=hs[c][:], in_=h_bf[c][:].rearrange("p n t -> p (n t)"))
+
+        def second(c):
+            zb[c] = psum.tile([P, PACK, CHUNK], F32, name="zb%d" % c)
+            for t in range(PACK):
+                nc.tensor.matmul_mx(out=zb[c][:, t, :], lhsT=w2w[:, 2 * t * P : 2 * (t + 1) * P].bitcast(FP4X4), lhsT_scale=w2s[:, t * P : (t + 1) * P],
+                                    rhs=hq[c][:].bitcast(FP8X4), rhs_scale=hs[c][:], start=True, stop=True)
+
+        def gate(c):
+            g[c] = keep.tile([P, PACK, CHUNK], F32, name="g%d" % c)
+            nc.scalar.activation(out=g[c][:], in_=zb[c][:], func=SIGMOID)
+
+        def product(c):
+            o32[c] = keep.tile([P, PACK, CHUNK], F32, name="o32_%d" % c)
+            nc.vector.tensor_tensor(out=o32[c][:], in0=hb[c][:], in1=g[c][:], op=MULT)
+            nc.sync.dma_start(out=out_rows[:, :, cols(c)], in_=o32[c][:])
+
+        def round_o(c):
+            o_bf[c] = keep.tile([P, CHUNK, PACK], BF16, name="o_bf%d" % c, align_bytes=64)
+            nc.vector.tensor_copy(out=o_bf[c][:].rearrange("p (n i) t -> p n t i", i=4), in_=o32[c][:].rearrange("p t (n i) -> p n t i", i=4))
+
+        def quant_o(c):
+            nc.vector.quantize_mx(out=oq[:, cols(c)].bitcast(FP8X4), scales=os_[:, cols(c)], in_=o_bf[c][:].rearrange("p n t -> p (n t)"))
+            nc.sync.dma_start(out=out_words[:, cols(c)], in_=oq[:, cols(c)].bitcast(I32))
+
+        w2w = keep.tile([P, 2 * H], U8, name="w2w", align_bytes=64)
+        w2s = keep.tile([P, H], U8, name="w2s", align_bytes=64)
+
+        def deal_w2():
+            nc.vector.tensor_copy(
+                out=w2w[:].rearrange("p (t m b) -> p m t b", t=PACK, b=2),
+                in_=w2w_raw[:].rearrange("p (m t b) -> p m t b", t=PACK, b=2),
+            )
+            nc.vector.tensor_copy(
+                out=w2s[:].rearrange("p (t m) -> p m t", t=PACK),
+                in_=w2s_raw[:].rearrange("p (m t) -> p m t", t=PACK),
+            )
+
+        steps = [gather, first, round_h, quant_h, second, gate, product, round_o, quant_o]
+        for s in range(CHUNKS + len(steps) - 1):
+            for k in reversed(range(len(steps))):
+                c = s - k
+                if 0 <= c < CHUNKS:
+                    steps[k](c)
+            if s == 1:
+                deal_w2()
+        scale_rows = out_2[0].bitcast(I32)
+        for q in range(4):
+            eng = nc.sync if q % 2 == 0 else nc.scalar
+            eng.dma_start(out=scale_rows[4 * q : 4 * q + 4, :], in_=os_[32 * q : 32 * q + 4, :].bitcast(I32))

@@ -27,20 +27,13 @@ def tile_picked_zgrn_lin_po_kernel(tc, x_words, x_scales, w1, w2_words, w2_scale
         keep = ctx.enter_context(tc.tile_pool(name="keep", bufs=1))
         psum = ctx.enter_context(tc.psum_pool(name="psum", bufs=1))
 
-        warm_in = keep.tile([P, 8], F32, name="warm_in")
-        warm_out = keep.tile([P, 8], F32, name="warm_out")
-        nc.gpsimd.memset(warm_in[:], 0.0)
-        nc.scalar.activation(out=warm_out[:], in_=warm_in[:], func=SIGMOID)
-
         offsets = keep.tile([P, S // 16], U16, name="offsets")
         nc.sync.dma_start(offsets[:], offs)
-
         xs_win = keep.tile([P, T], U8, name="xs_win", align_bytes=64)
+        nc.vector.memset(xs_win[:].bitcast(I32), 0)
         for q in range(4):
-            nc.sync.dma_start(
-                out=xs_win[32 * q : 32 * q + 32, :].bitcast(I32),
-                in_=x_scales[0, 4 * q : 4 * q + 4, :].bitcast(I32).unsqueeze(0).broadcast_to([8, 4, T // 4]),
-            )
+            nc.scalar.dma_start(out=xs_win[32 * q : 32 * q + 4, :].bitcast(I32), in_=x_scales[0, 4 * q : 4 * q + 4, :].bitcast(I32))
+
         w1_rows = w1.rearrange("(p j) c -> p j c", j=PACK)
         w1_raw = []
         for h in range(2):
@@ -50,23 +43,40 @@ def tile_picked_zgrn_lin_po_kernel(tc, x_words, x_scales, w1, w2_words, w2_scale
         xw_win = keep.tile([P, T], I32, name="xw_win", align_bytes=64)
         nc.sync.dma_start(out=xw_win[:], in_=x_words[0].rearrange("p c r -> p (c r)").bitcast(I32))
 
+        warm_in = keep.tile([P, 8], F32, name="warm_in")
+        warm_out = keep.tile([P, 8], F32, name="warm_out", tag="w2_words", align_bytes=64)
+        nc.vector.memset(warm_in[:], 0.0)
+        nc.scalar.activation(out=warm_out[:], in_=warm_in[:], func=SIGMOID)
+
+        w2w_raw = keep.tile([P, 2 * H], U8, name="w2w_raw", tag="w2_words", align_bytes=64)
+        nc.scalar.dma_start(out=w2w_raw[:].bitcast(I32), in_=w2_words[0].bitcast(I32))
         w2s_raw = keep.tile([P, H], U8, name="w2s_raw", align_bytes=64)
+        nc.vector.memset(w2s_raw[:].bitcast(I32), 0)
         for q in range(4):
-            nc.sync.dma_start(
-                out=w2s_raw[32 * q : 32 * q + 32, :].bitcast(I32),
-                in_=w2_scales[0, 4 * q : 4 * q + 4, :].bitcast(I32).unsqueeze(0).broadcast_to([8, 4, H // 4]),
-            )
-        w2w_raw = keep.tile([P, 2 * H], U8, name="w2w_raw", align_bytes=64)
-        nc.sync.dma_start(out=w2w_raw[:].bitcast(I32), in_=w2_words[0].bitcast(I32))
+            nc.scalar.dma_start(out=w2s_raw[32 * q : 32 * q + 4, :].bitcast(I32), in_=w2_scales[0, 4 * q : 4 * q + 4, :].bitcast(I32))
 
         xs = keep.tile([P, S], U8, name="xs", align_bytes=64)
         nc.vector.tensor_copy(xs[:], xs_win[:].indirect(offsets[:]))
+
+        w2w = keep.tile([P, 2 * H], U8, name="w2w", align_bytes=64)
+        nc.vector.tensor_copy(
+            out=w2w[:].rearrange("p (t m b) -> p m t b", t=PACK, b=2),
+            in_=w2w_raw[:].rearrange("p (m t b) -> p m t b", t=PACK, b=2),
+        )
+        w2s = keep.tile([P, H], U8, name="w2s", align_bytes=64)
+        nc.vector.tensor_copy(
+            out=w2s[:].rearrange("p (t m) -> p m t", t=PACK),
+            in_=w2s_raw[:].rearrange("p (m t) -> p m t", t=PACK),
+        )
 
         w1_bf = keep.tile([P, H * PACK], BF16, name="w1_bf", align_bytes=64)
         w1_dealt = w1_bf[:].rearrange("p (t m j) -> p m j t", t=PACK, j=PACK)
         half = P // 2
         nc.scalar.copy(out=w1_dealt[:, 0:half], in_=w1_raw[0][:].rearrange("p j (m t) -> p m j t", t=PACK))
-        nc.vector.tensor_copy(out=w1_dealt[:, half:P], in_=w1_raw[1][:].rearrange("p j (m t) -> p m j t", t=PACK))
+        second_half = w1_raw[1][:].rearrange("p j (m t) -> p m j t", t=PACK)
+        cut = 42
+        nc.vector.tensor_copy(out=w1_dealt[:, half : half + cut], in_=second_half[:, 0:cut])
+        nc.scalar.copy(out=w1_dealt[:, half + cut : P], in_=second_half[:, cut:half])
         w1q = keep.tile([P, H], U32, name="w1q", align_bytes=64)
         w1s = keep.tile([P, H], U8, name="w1s", align_bytes=64)
         nc.vector.quantize_mx(out=w1q[:].bitcast(FP8X4), scales=w1s[:], in_=w1_bf[:])
@@ -93,7 +103,8 @@ def tile_picked_zgrn_lin_po_kernel(tc, x_words, x_scales, w1, w2_words, w2_scale
 
         def round_h(c):
             h_bf[c] = keep.tile([P, CHUNK, PACK], BF16, name="h_bf%d" % c, align_bytes=64)
-            nc.scalar.copy(out=h_bf[c][:], in_=hb[c][:].rearrange("p t n -> p n t"))
+            copy = nc.vector.tensor_copy if c == CHUNKS - 1 else nc.scalar.copy
+            copy(out=h_bf[c][:], in_=hb[c][:].rearrange("p t n -> p n t"))
 
         def quant_h(c):
             hq[c] = keep.tile([P, CHUNK], U32, name="hq%d" % c, align_bytes=64)
@@ -117,34 +128,20 @@ def tile_picked_zgrn_lin_po_kernel(tc, x_words, x_scales, w1, w2_words, w2_scale
 
         def round_o(c):
             o_bf[c] = keep.tile([P, CHUNK, PACK], BF16, name="o_bf%d" % c, align_bytes=64)
-            nc.vector.tensor_copy(out=o_bf[c][:].rearrange("p (n i) t -> p n t i", i=4), in_=o32[c][:].rearrange("p t (n i) -> p n t i", i=4))
+            copy = nc.scalar.copy if c < 2 else nc.vector.tensor_copy
+            copy(out=o_bf[c][:].rearrange("p (n i) t -> p n t i", i=4), in_=o32[c][:].rearrange("p t (n i) -> p n t i", i=4))
 
         def quant_o(c):
             nc.vector.quantize_mx(out=oq[:, cols(c)].bitcast(FP8X4), scales=os_[:, cols(c)], in_=o_bf[c][:].rearrange("p n t -> p (n t)"))
-            nc.sync.dma_start(out=out_words[:, cols(c)], in_=oq[:, cols(c)].bitcast(I32))
+            if c % 2 == 1:
+                both = slice((c - 1) * CHUNK, (c + 1) * CHUNK)
+                nc.scalar.dma_start(out=out_words[:, both], in_=oq[:, both].bitcast(I32))
 
-        w2w = keep.tile([P, 2 * H], U8, name="w2w", align_bytes=64)
-        w2s = keep.tile([P, H], U8, name="w2s", align_bytes=64)
-
-        def deal_w2():
-            nc.vector.tensor_copy(
-                out=w2w[:].rearrange("p (t m b) -> p m t b", t=PACK, b=2),
-                in_=w2w_raw[:].rearrange("p (m t b) -> p m t b", t=PACK, b=2),
-            )
-            nc.vector.tensor_copy(
-                out=w2s[:].rearrange("p (t m) -> p m t", t=PACK),
-                in_=w2s_raw[:].rearrange("p (m t) -> p m t", t=PACK),
-            )
-
-        steps = [gather, first, round_h, quant_h, second, gate, product, round_o, quant_o]
-        for s in range(CHUNKS + len(steps) - 1):
-            for k in reversed(range(len(steps))):
-                c = s - k
-                if 0 <= c < CHUNKS:
-                    steps[k](c)
-            if s == 1:
-                deal_w2()
+        for group in ((gather, first, round_h, quant_h, second), (gate, product), (round_o, quant_o)):
+            for c in range(CHUNKS):
+                for step in group:
+                    step(c)
         scale_rows = out_2[0].bitcast(I32)
         for q in range(4):
-            eng = nc.sync if q % 2 == 0 else nc.scalar
+            eng = nc.sync if q < 3 else nc.scalar
             eng.dma_start(out=scale_rows[4 * q : 4 * q + 4, :], in_=os_[32 * q : 32 * q + 4, :].bitcast(I32))

@@ -25,15 +25,22 @@ def tile_picked_zgrn_lin_po_kernel(tc, x_words, x_scales, w1, w2_words, w2_scale
     nc = tc.nc
     with ExitStack() as ctx:
         keep = ctx.enter_context(tc.tile_pool(name="keep", bufs=1))
+        reuse = ctx.enter_context(tc.tile_pool(name="reuse", bufs=1))
         psum = ctx.enter_context(tc.psum_pool(name="psum", bufs=1))
+
+        warm_in = keep.tile([P, 8], F32, name="warm_in")
+        warm_out = keep.tile([P, 8], F32, name="warm_out")
+        nc.vector.memset(warm_in[:], 0.0)
+        nc.scalar.activation(out=warm_out[:], in_=warm_in[:], func=SIGMOID)
 
         offsets = keep.tile([P, S // 16], U16, name="offsets")
         nc.sync.dma_start(offsets[:], offs)
         xs_win = keep.tile([P, T], U8, name="xs_win", align_bytes=64)
-        nc.vector.memset(xs_win[:].bitcast(I32), 0)
         for q in range(4):
-            nc.scalar.dma_start(out=xs_win[32 * q : 32 * q + 4, :].bitcast(I32), in_=x_scales[0, 4 * q : 4 * q + 4, :].bitcast(I32))
-
+            nc.sync.dma_start(
+                out=xs_win[32 * q : 32 * q + 32, :].bitcast(I32),
+                in_=x_scales[0, 4 * q : 4 * q + 4, :].bitcast(I32).unsqueeze(0).broadcast_to([8, 4, T // 4]),
+            )
         w1_rows = w1.rearrange("(p j) c -> p j c", j=PACK)
         w1_raw = []
         for h in range(2):
@@ -42,44 +49,41 @@ def tile_picked_zgrn_lin_po_kernel(tc, x_words, x_scales, w1, w2_words, w2_scale
             w1_raw.append(raw)
         xw_win = keep.tile([P, T], I32, name="xw_win", align_bytes=64)
         nc.sync.dma_start(out=xw_win[:], in_=x_words[0].rearrange("p c r -> p (c r)").bitcast(I32))
-
-        warm_in = keep.tile([P, 8], F32, name="warm_in")
-        warm_out = keep.tile([P, 8], F32, name="warm_out", tag="w2_words", align_bytes=64)
-        nc.vector.memset(warm_in[:], 0.0)
-        nc.scalar.activation(out=warm_out[:], in_=warm_in[:], func=SIGMOID)
-
-        w2w_raw = keep.tile([P, 2 * H], U8, name="w2w_raw", tag="w2_words", align_bytes=64)
-        nc.scalar.dma_start(out=w2w_raw[:].bitcast(I32), in_=w2_words[0].bitcast(I32))
-        w2s_raw = keep.tile([P, H], U8, name="w2s_raw", align_bytes=64)
+        w2w_raw = keep.tile([P, 2 * H], U8, name="w2w_raw", align_bytes=64)
+        nc.sync.dma_start(out=w2w_raw[:].bitcast(I32), in_=w2_words[0].bitcast(I32))
+        w2s_raw = reuse.tile([P, H], U8, name="w2s_raw", align_bytes=64, offset=0)
         nc.vector.memset(w2s_raw[:].bitcast(I32), 0)
         for q in range(4):
-            nc.scalar.dma_start(out=w2s_raw[32 * q : 32 * q + 4, :].bitcast(I32), in_=w2_scales[0, 4 * q : 4 * q + 4, :].bitcast(I32))
+            nc.sync.dma_start(out=w2s_raw[32 * q : 32 * q + 4, :].bitcast(I32), in_=w2_scales[0, 4 * q : 4 * q + 4, :].bitcast(I32))
 
         xs = keep.tile([P, S], U8, name="xs", align_bytes=64)
         nc.vector.tensor_copy(xs[:], xs_win[:].indirect(offsets[:]))
 
         w2w = keep.tile([P, 2 * H], U8, name="w2w", align_bytes=64)
-        nc.vector.tensor_copy(
-            out=w2w[:].rearrange("p (t m b) -> p m t b", t=PACK, b=2),
-            in_=w2w_raw[:].rearrange("p (m t b) -> p m t b", t=PACK, b=2),
-        )
-        w2s = keep.tile([P, H], U8, name="w2s", align_bytes=64)
-        nc.vector.tensor_copy(
-            out=w2s[:].rearrange("p (t m) -> p m t", t=PACK),
-            in_=w2s_raw[:].rearrange("p (m t) -> p m t", t=PACK),
-        )
-
         w1_bf = keep.tile([P, H * PACK], BF16, name="w1_bf", align_bytes=64)
         w1_dealt = w1_bf[:].rearrange("p (t m j) -> p m j t", t=PACK, j=PACK)
         half = P // 2
         nc.scalar.copy(out=w1_dealt[:, 0:half], in_=w1_raw[0][:].rearrange("p j (m t) -> p m j t", t=PACK))
         second_half = w1_raw[1][:].rearrange("p j (m t) -> p m j t", t=PACK)
-        cut = 42
-        nc.vector.tensor_copy(out=w1_dealt[:, half : half + cut], in_=second_half[:, 0:cut])
-        nc.scalar.copy(out=w1_dealt[:, half + cut : P], in_=second_half[:, cut:half])
+        nc.vector.tensor_copy(out=w1_dealt[:, half:P, :, 0:2], in_=second_half[:, :, :, 0:2])
+        nc.scalar.copy(out=w1_dealt[:, half:P, :, 2:4], in_=second_half[:, :, :, 2:4])
+        w2s = keep.tile([P, H], U8, name="w2s", align_bytes=64)
+
+        def deal_scales():
+            nc.vector.tensor_copy(
+                out=w2w[:].rearrange("p (t m b) -> p m t b", t=PACK, b=2),
+                in_=w2w_raw[:].rearrange("p (m t b) -> p m t b", t=PACK, b=2),
+            )
+            nc.vector.tensor_copy(
+                out=w2s[:].rearrange("p (t m) -> p m t", t=PACK),
+                in_=w2s_raw[:].rearrange("p (m t) -> p m t", t=PACK),
+            )
+
         w1q = keep.tile([P, H], U32, name="w1q", align_bytes=64)
         w1s = keep.tile([P, H], U8, name="w1s", align_bytes=64)
-        nc.vector.quantize_mx(out=w1q[:].bitcast(FP8X4), scales=w1s[:], in_=w1_bf[:])
+        for u in range(2):
+            part = slice(u * 2 * P, (u + 1) * 2 * P)
+            nc.vector.quantize_mx(out=w1q[:, part].bitcast(FP8X4), scales=w1s[:, part], in_=w1_bf[:, u * 2 * P * PACK : (u + 1) * 2 * P * PACK])
 
         oq = keep.tile([P, S], U32, name="oq", align_bytes=64)
         os_ = keep.tile([P, S], U8, name="os_", align_bytes=64)
@@ -102,13 +106,13 @@ def tile_picked_zgrn_lin_po_kernel(tc, x_words, x_scales, w1, w2_words, w2_scale
                                     rhs=xw[c][:].bitcast(FP8X4), rhs_scale=xs[:, cols(c)], start=True, stop=True)
 
         def round_h(c):
-            h_bf[c] = keep.tile([P, CHUNK, PACK], BF16, name="h_bf%d" % c, align_bytes=64)
+            h_bf[c] = keep.tile([P, CHUNK, PACK], BF16, name="h_bf%d" % c, tag="h_bf", bufs=2, align_bytes=64)
             copy = nc.vector.tensor_copy if c == CHUNKS - 1 else nc.scalar.copy
             copy(out=h_bf[c][:], in_=hb[c][:].rearrange("p t n -> p n t"))
 
         def quant_h(c):
             hq[c] = keep.tile([P, CHUNK], U32, name="hq%d" % c, align_bytes=64)
-            hs[c] = keep.tile([P, CHUNK], U8, name="hs%d" % c, align_bytes=64)
+            hs[c] = reuse.tile([P, CHUNK], U8, name="hs%d" % c, align_bytes=64, offset=c * CHUNK)
             nc.vector.quantize_mx(out=hq[c][:].bitcast(FP8X4), scales=hs[c][:], in_=h_bf[c][:].rearrange("p n t -> p (n t)"))
 
         def second(c):
@@ -128,7 +132,7 @@ def tile_picked_zgrn_lin_po_kernel(tc, x_words, x_scales, w1, w2_words, w2_scale
 
         def round_o(c):
             o_bf[c] = keep.tile([P, CHUNK, PACK], BF16, name="o_bf%d" % c, align_bytes=64)
-            copy = nc.scalar.copy if c < 2 else nc.vector.tensor_copy
+            copy = nc.scalar.copy if c in (0, 1) else nc.vector.tensor_copy
             copy(out=o_bf[c][:].rearrange("p (n i) t -> p n t i", i=4), in_=o32[c][:].rearrange("p t (n i) -> p n t i", i=4))
 
         def quant_o(c):
@@ -141,6 +145,8 @@ def tile_picked_zgrn_lin_po_kernel(tc, x_words, x_scales, w1, w2_words, w2_scale
             for c in range(CHUNKS):
                 for step in group:
                     step(c)
+                    if step is round_h and c == 0:
+                        deal_scales()
         scale_rows = out_2[0].bitcast(I32)
         for q in range(4):
             eng = nc.sync if q < 3 else nc.scalar

@@ -71,12 +71,12 @@ def tile_picked_zgrn_lin_po_kernel(tc, x_words, x_scales, w1, w2_words, w2_scale
 
         def deal_scales():
             nc.vector.tensor_copy(
-                out=w2w[:].rearrange("p (t m b) -> p m t b", t=PACK, b=2),
-                in_=w2w_raw[:].rearrange("p (m t b) -> p m t b", t=PACK, b=2),
+                out=w2w[:].rearrange("p (t m b) -> p t m b", t=PACK, b=2),
+                in_=w2w_raw[:].rearrange("p (m t b) -> p t m b", t=PACK, b=2),
             )
             nc.vector.tensor_copy(
-                out=w2s[:].rearrange("p (t m) -> p m t", t=PACK),
-                in_=w2s_raw[:].rearrange("p (m t) -> p m t", t=PACK),
+                out=w2s[:].rearrange("p (t m) -> p t m", t=PACK),
+                in_=w2s_raw[:].rearrange("p (m t) -> p t m", t=PACK),
             )
 
         w1q = keep.tile([P, H], U32, name="w1q", align_bytes=64)
@@ -115,25 +115,35 @@ def tile_picked_zgrn_lin_po_kernel(tc, x_words, x_scales, w1, w2_words, w2_scale
             hs[c] = reuse.tile([P, CHUNK], U8, name="hs%d" % c, align_bytes=64, offset=c * CHUNK)
             nc.vector.quantize_mx(out=hq[c][:].bitcast(FP8X4), scales=hs[c][:], in_=h_bf[c][:].rearrange("p n t -> p (n t)"))
 
+        def parts(c):
+            return ((0, 2), (2, 4)) if c == 0 else ((0, 4),)
+
         def second(c):
-            zb[c] = psum.tile([P, PACK, CHUNK], F32, name="zb%d" % c)
-            for t in range(PACK):
-                nc.tensor.matmul_mx(out=zb[c][:, t, :], lhsT=w2w[:, 2 * t * P : 2 * (t + 1) * P].bitcast(FP4X4), lhsT_scale=w2s[:, t * P : (t + 1) * P],
-                                    rhs=hq[c][:].bitcast(FP8X4), rhs_scale=hs[c][:], start=True, stop=True)
+            for lo, hi in parts(c):
+                zb[c, lo] = psum.tile([P, hi - lo, CHUNK], F32, name="zb%d_%d" % (c, lo), tag="zb%d_%d" % (c % 3, lo))
+                for t in range(lo, hi):
+                    nc.tensor.matmul_mx(out=zb[c, lo][:, t - lo, :], lhsT=w2w[:, 2 * t * P : 2 * (t + 1) * P].bitcast(FP4X4), lhsT_scale=w2s[:, t * P : (t + 1) * P],
+                                        rhs=hq[c][:].bitcast(FP8X4), rhs_scale=hs[c][:], start=True, stop=True)
 
         def gate(c):
             g[c] = keep.tile([P, PACK, CHUNK], F32, name="g%d" % c)
-            nc.scalar.activation(out=g[c][:], in_=zb[c][:], func=SIGMOID)
+            for lo, hi in parts(c):
+                nc.scalar.activation(out=g[c][:, lo:hi, :], in_=zb[c, lo][:], func=SIGMOID)
 
         def product(c):
             o32[c] = keep.tile([P, PACK, CHUNK], F32, name="o32_%d" % c)
-            nc.vector.tensor_tensor(out=o32[c][:], in0=hb[c][:], in1=g[c][:], op=MULT)
-            nc.sync.dma_start(out=out_rows[:, :, cols(c)], in_=o32[c][:])
+            for lo, hi in parts(c):
+                nc.vector.tensor_tensor(out=o32[c][:, lo:hi, :], in0=hb[c][:, lo:hi, :], in1=g[c][:, lo:hi, :], op=MULT)
+                nc.sync.dma_start(out=out_rows[:, lo:hi, cols(c)], in_=o32[c][:, lo:hi, :])
 
         def round_o(c):
             o_bf[c] = keep.tile([P, CHUNK, PACK], BF16, name="o_bf%d" % c, align_bytes=64)
-            copy = nc.scalar.copy if c in (0, 1) else nc.vector.tensor_copy
-            copy(out=o_bf[c][:].rearrange("p (n i) t -> p n t i", i=4), in_=o32[c][:].rearrange("p t (n i) -> p n t i", i=4))
+            dst = o_bf[c][:].rearrange("p (n i) t -> p n t i", i=4)
+            src = o32[c][:].rearrange("p t (n i) -> p n t i", i=4)
+            if c < 2:
+                nc.scalar.copy(out=dst, in_=src)
+            else:
+                nc.vector.tensor_copy(out=dst, in_=src)
 
         def quant_o(c):
             nc.vector.quantize_mx(out=oq[:, cols(c)].bitcast(FP8X4), scales=os_[:, cols(c)], in_=o_bf[c][:].rearrange("p n t -> p (n t)"))

@@ -28,6 +28,8 @@ def tile_picked_zgrn_lin_po_kernel(tc, x_words, x_scales, w1, w2_words, w2_scale
         reuse = ctx.enter_context(tc.tile_pool(name="reuse", bufs=1))
         psum = ctx.enter_context(tc.psum_pool(name="psum", bufs=1))
 
+        xs_win = keep.tile([P, T], U8, name="xs_win", align_bytes=64)
+        nc.vector.memset(xs_win[:].bitcast(I32), 0)
         warm_in = keep.tile([P, 8], F32, name="warm_in")
         warm_out = keep.tile([P, 8], F32, name="warm_out")
         nc.vector.memset(warm_in[:], 0.0)
@@ -35,18 +37,15 @@ def tile_picked_zgrn_lin_po_kernel(tc, x_words, x_scales, w1, w2_words, w2_scale
 
         offsets = keep.tile([P, S // 16], U16, name="offsets")
         nc.sync.dma_start(offsets[:], offs)
-        xs_win = keep.tile([P, T], U8, name="xs_win", align_bytes=64)
-        for q in range(4):
-            nc.sync.dma_start(
-                out=xs_win[32 * q : 32 * q + 32, :].bitcast(I32),
-                in_=x_scales[0, 4 * q : 4 * q + 4, :].bitcast(I32).unsqueeze(0).broadcast_to([8, 4, T // 4]),
-            )
         w1_rows = w1.rearrange("(p j) c -> p j c", j=PACK)
         w1_raw = []
         for h in range(2):
             raw = keep.tile([P, PACK, H // 2], F32, name="w1_raw%d" % h)
             nc.sync.dma_start(out=raw[:], in_=w1_rows[:, :, h * (H // 2) : (h + 1) * (H // 2)])
             w1_raw.append(raw)
+            if h == 0:
+                for q in range(4):
+                    nc.sync.dma_start(out=xs_win[32 * q : 32 * q + 4, :].bitcast(I32), in_=x_scales[0, 4 * q : 4 * q + 4, :].bitcast(I32))
         xw_win = keep.tile([P, T], I32, name="xw_win", align_bytes=64)
         nc.sync.dma_start(out=xw_win[:], in_=x_words[0].rearrange("p c r -> p (c r)").bitcast(I32))
         w2w_raw = keep.tile([P, 2 * H], U8, name="w2w_raw", align_bytes=64)

@@ -46,10 +46,10 @@ def tile_picked_zgrn_lin_po_kernel(tc, x_words, x_scales, w1, w2_words, w2_scale
             if h == 0:
                 for q in range(4):
                     nc.sync.dma_start(out=xs_win[32 * q : 32 * q + 4, :].bitcast(I32), in_=x_scales[0, 4 * q : 4 * q + 4, :].bitcast(I32))
+                w2w_raw = keep.tile([P, 2 * H], U8, name="w2w_raw", align_bytes=64)
+                nc.sync.dma_start(out=w2w_raw[:].bitcast(I32), in_=w2_words[0].bitcast(I32))
         xw_win = keep.tile([P, T], I32, name="xw_win", align_bytes=64)
         nc.sync.dma_start(out=xw_win[:], in_=x_words[0].rearrange("p c r -> p (c r)").bitcast(I32))
-        w2w_raw = keep.tile([P, 2 * H], U8, name="w2w_raw", align_bytes=64)
-        nc.sync.dma_start(out=w2w_raw[:].bitcast(I32), in_=w2_words[0].bitcast(I32))
         w2s_raw = reuse.tile([P, H], U8, name="w2s_raw", align_bytes=64, offset=0)
         nc.vector.memset(w2s_raw[:].bitcast(I32), 0)
         for q in range(4):
@@ -59,20 +59,20 @@ def tile_picked_zgrn_lin_po_kernel(tc, x_words, x_scales, w1, w2_words, w2_scale
         nc.vector.tensor_copy(xs[:], xs_win[:].indirect(offsets[:]))
 
         w2w = keep.tile([P, 2 * H], U8, name="w2w", align_bytes=64)
+        nc.vector.tensor_copy(
+            out=w2w[:].bitcast(U16).rearrange("p (t m) -> p t m", t=PACK),
+            in_=w2w_raw[:].bitcast(U16).rearrange("p (m t) -> p t m", t=PACK),
+        )
         w1_bf = keep.tile([P, H * PACK], BF16, name="w1_bf", align_bytes=64)
         w1_dealt = w1_bf[:].rearrange("p (t m j) -> p m j t", t=PACK, j=PACK)
         half = P // 2
         nc.scalar.copy(out=w1_dealt[:, 0:half], in_=w1_raw[0][:].rearrange("p j (m t) -> p m j t", t=PACK))
         second_half = w1_raw[1][:].rearrange("p j (m t) -> p m j t", t=PACK)
-        nc.vector.tensor_copy(out=w1_dealt[:, half:P, :, 0:2], in_=second_half[:, :, :, 0:2])
+        nc.scalar.copy(out=w1_dealt[:, half:P, :, 0:2], in_=second_half[:, :, :, 0:2])
         nc.scalar.copy(out=w1_dealt[:, half:P, :, 2:4], in_=second_half[:, :, :, 2:4])
         w2s = keep.tile([P, H], U8, name="w2s", align_bytes=64)
 
         def deal_scales():
-            nc.vector.tensor_copy(
-                out=w2w[:].rearrange("p (t m b) -> p t m b", t=PACK, b=2),
-                in_=w2w_raw[:].rearrange("p (m t b) -> p t m b", t=PACK, b=2),
-            )
             nc.vector.tensor_copy(
                 out=w2s[:].rearrange("p (t m) -> p t m", t=PACK),
                 in_=w2s_raw[:].rearrange("p (m t) -> p t m", t=PACK),
@@ -80,7 +80,8 @@ def tile_picked_zgrn_lin_po_kernel(tc, x_words, x_scales, w1, w2_words, w2_scale
 
         w1q = keep.tile([P, H], U32, name="w1q", align_bytes=64)
         w1s = keep.tile([P, H], U8, name="w1s", align_bytes=64)
-        for u in range(2):
+
+        def quant_w1(u):
             part = slice(u * 2 * P, (u + 1) * 2 * P)
             nc.vector.quantize_mx(out=w1q[:, part].bitcast(FP8X4), scales=w1s[:, part], in_=w1_bf[:, u * 2 * P * PACK : (u + 1) * 2 * P * PACK])
 
@@ -150,12 +151,19 @@ def tile_picked_zgrn_lin_po_kernel(tc, x_words, x_scales, w1, w2_words, w2_scale
                 both = slice((c - 1) * CHUNK, (c + 1) * CHUNK)
                 nc.scalar.dma_start(out=out_words[:, both], in_=oq[:, both].bitcast(I32))
 
-        for group in ((gather, first, round_h, quant_h, second), (gate, product), (round_o, quant_o)):
+        quant_w1(0)
+        gather(0)
+        quant_w1(1)
+        first(0)
+        for c in range(1, CHUNKS):
+            if c == CHUNKS - 1:
+                deal_scales()
+            gather(c)
+            first(c)
+        for group in ((round_h, quant_h, second), (gate, product), (round_o, quant_o)):
             for c in range(CHUNKS):
                 for step in group:
                     step(c)
-                    if step is round_h and c == 0:
-                        deal_scales()
         scale_rows = out_2[0].bitcast(I32)
         for q in range(4):
             eng = nc.sync if q < 3 else nc.scalar

@@ -36,7 +36,6 @@ def tile_picked_zgrn_lin_po_kernel(tc, x_words, x_scales, w1, w2_words, w2_scale
         nc.scalar.activation(out=warm_out[:], in_=warm_in[:], func=SIGMOID)
 
         offsets = keep.tile([P, S // 16], U16, name="offsets")
-        nc.sync.dma_start(offsets[:], offs)
         w1_rows = w1.rearrange("(p j) c -> p j c", j=PACK)
         w1_raw = []
         for h in range(2):
@@ -44,12 +43,13 @@ def tile_picked_zgrn_lin_po_kernel(tc, x_words, x_scales, w1, w2_words, w2_scale
             nc.sync.dma_start(out=raw[:], in_=w1_rows[:, :, h * (H // 2) : (h + 1) * (H // 2)])
             w1_raw.append(raw)
             if h == 0:
+                nc.sync.dma_start(offsets[:], offs)
                 for q in range(4):
                     nc.sync.dma_start(out=xs_win[32 * q : 32 * q + 4, :].bitcast(I32), in_=x_scales[0, 4 * q : 4 * q + 4, :].bitcast(I32))
-                w2w_raw = keep.tile([P, 2 * H], U8, name="w2w_raw", align_bytes=64)
-                nc.sync.dma_start(out=w2w_raw[:].bitcast(I32), in_=w2_words[0].bitcast(I32))
         xw_win = keep.tile([P, T], I32, name="xw_win", align_bytes=64)
         nc.sync.dma_start(out=xw_win[:], in_=x_words[0].rearrange("p c r -> p (c r)").bitcast(I32))
+        w2w_raw = keep.tile([P, 2 * H], U8, name="w2w_raw", align_bytes=64)
+        nc.sync.dma_start(out=w2w_raw[:].bitcast(I32), in_=w2_words[0].bitcast(I32))
         w2s_raw = reuse.tile([P, H], U8, name="w2s_raw", align_bytes=64, offset=0)
         nc.vector.memset(w2s_raw[:].bitcast(I32), 0)
         for q in range(4):
@@ -59,10 +59,6 @@ def tile_picked_zgrn_lin_po_kernel(tc, x_words, x_scales, w1, w2_words, w2_scale
         nc.vector.tensor_copy(xs[:], xs_win[:].indirect(offsets[:]))
 
         w2w = keep.tile([P, 2 * H], U8, name="w2w", align_bytes=64)
-        nc.vector.tensor_copy(
-            out=w2w[:].bitcast(U16).rearrange("p (t m) -> p t m", t=PACK),
-            in_=w2w_raw[:].bitcast(U16).rearrange("p (m t) -> p t m", t=PACK),
-        )
         w1_bf = keep.tile([P, H * PACK], BF16, name="w1_bf", align_bytes=64)
         w1_dealt = w1_bf[:].rearrange("p (t m j) -> p m j t", t=PACK, j=PACK)
         half = P // 2
@@ -73,6 +69,10 @@ def tile_picked_zgrn_lin_po_kernel(tc, x_words, x_scales, w1, w2_words, w2_scale
         w2s = keep.tile([P, H], U8, name="w2s", align_bytes=64)
 
         def deal_scales():
+            nc.vector.tensor_copy(
+                out=w2w[:].bitcast(U16).rearrange("p (t m) -> p t m", t=PACK),
+                in_=w2w_raw[:].bitcast(U16).rearrange("p (m t) -> p t m", t=PACK),
+            )
             nc.vector.tensor_copy(
                 out=w2s[:].rearrange("p (t m) -> p t m", t=PACK),
                 in_=w2s_raw[:].rearrange("p (m t) -> p t m", t=PACK),

@@ -12,12 +12,15 @@ FP8X4 = mybir.dt.float8_e4m3fn_x4
 FP4X4 = mybir.dt.float4_e2m1fn_x4
 SIGMOID = mybir.ActivationFunctionType.Sigmoid
 MULT = mybir.AluOpType.mult
+ADD = mybir.AluOpType.add
 
 P = 128
 PACK = 4
 K, T, S, H = 512, 1024, 512, 512
 CHUNK = 128
 CHUNKS = S // CHUNK
+WARM_M = 32
+WARM_PASSES = 12
 FLOPS = 2 * K * H * S + 2 * H * H * S
 
 
@@ -56,7 +59,18 @@ def tile_picked_zgrn_lin_po_kernel(tc, x_words, x_scales, w1, w2_words, w2_scale
             nc.sync.dma_start(out=w2s_raw[32 * q : 32 * q + 4, :].bitcast(I32), in_=w2_scales[0, 4 * q : 4 * q + 4, :].bitcast(I32))
 
         xs = keep.tile([P, S], U8, name="xs", align_bytes=64)
-        nc.vector.tensor_copy(xs[:], xs_win[:].indirect(offsets[:]))
+        nc.vector.tensor_copy(xs[:, 0:CHUNK], xs_win[:].indirect(offsets[:, 0 : CHUNK // 16]))
+        nc.vector.tensor_copy(xs[:, CHUNK:S], xs_win[:].indirect(offsets[:, CHUNK // 16 : S // 16]))
+
+        ones = keep.tile([P, CHUNK * PACK], BF16, name="ones", align_bytes=64)
+        nc.vector.memset(ones[:], 1.0)
+        ones_q = keep.tile([P, CHUNK], U32, name="ones_q", align_bytes=64)
+        ones_s = keep.tile([P, CHUNK], U8, name="ones_s", align_bytes=64)
+        nc.vector.quantize_mx(out=ones_q[:].bitcast(FP8X4), scales=ones_s[:], in_=ones[:])
+        warm_bank = psum.tile([WARM_M, CHUNK], F32, name="warm_bank", tag="zb1_0")
+        for n_pass in range(WARM_PASSES):
+            nc.tensor.matmul_mx(out=warm_bank[:], lhsT=ones_q[:, 0:WARM_M].bitcast(FP8X4), lhsT_scale=ones_s[:, 0:WARM_M],
+                                rhs=ones_q[:].bitcast(FP8X4), rhs_scale=xs[:, 0:CHUNK], start=True, stop=True)
 
         w2w = keep.tile([P, 2 * H], U8, name="w2w", align_bytes=64)
         w1_bf = keep.tile([P, H * PACK], BF16, name="w1_bf", align_bytes=64)
@@ -125,42 +139,54 @@ def tile_picked_zgrn_lin_po_kernel(tc, x_words, x_scales, w1, w2_words, w2_scale
                     nc.tensor.matmul_mx(out=zb[c, lo][:, t - lo, :], lhsT=w2w[:, 2 * t * P : 2 * (t + 1) * P].bitcast(FP4X4), lhsT_scale=w2s[:, t * P : (t + 1) * P],
                                         rhs=hq[c][:].bitcast(FP8X4), rhs_scale=hs[c][:], start=True, stop=True)
 
+        def spans(c):
+            return (slice(0, CHUNK),) if c == 0 else (slice(0, CHUNK // 2), slice(CHUNK // 2, CHUNK))
+
         def gate(c):
             g[c] = keep.tile([P, PACK, CHUNK], F32, name="g%d" % c)
             for lo, hi in parts(c):
-                nc.scalar.activation(out=g[c][:, lo:hi, :], in_=zb[c, lo][:], func=SIGMOID)
+                for n in spans(c):
+                    nc.scalar.activation(out=g[c][:, lo:hi, n], in_=zb[c, lo][:, :, n], func=SIGMOID)
 
         def product(c):
             o32[c] = keep.tile([P, PACK, CHUNK], F32, name="o32_%d" % c)
             for lo, hi in parts(c):
-                nc.vector.tensor_tensor(out=o32[c][:, lo:hi, :], in0=hb[c][:, lo:hi, :], in1=g[c][:, lo:hi, :], op=MULT)
+                for n in spans(c):
+                    nc.vector.tensor_tensor(out=o32[c][:, lo:hi, n], in0=hb[c][:, lo:hi, n], in1=g[c][:, lo:hi, n], op=MULT)
                 nc.sync.dma_start(out=out_rows[:, lo:hi, cols(c)], in_=o32[c][:, lo:hi, :])
 
         def round_o(c):
             o_bf[c] = keep.tile([P, CHUNK, PACK], BF16, name="o_bf%d" % c, align_bytes=64)
             dst = o_bf[c][:].rearrange("p (n i) t -> p n t i", i=4)
             src = o32[c][:].rearrange("p t (n i) -> p n t i", i=4)
+            cut = CHUNK // 8
             if c < 2:
+                n = CHUNK if c == 0 else CHUNK // 2
+                nc.gpsimd.tensor_scalar(out=o_bf[c][:, 0:n], in0=o32[c][:].rearrange("p t n -> p n t")[:, 0:n], scalar1=1.0, scalar2=0.0, op0=MULT, op1=ADD)
+                if c == 1:
+                    nc.scalar.copy(out=dst[:, cut:], in_=src[:, cut:])
+            elif c == 2:
                 nc.scalar.copy(out=dst, in_=src)
             else:
-                nc.vector.tensor_copy(out=dst, in_=src)
+                nc.scalar.copy(out=dst[:, 0:cut], in_=src[:, 0:cut])
+                nc.vector.tensor_copy(out=dst[:, cut:], in_=src[:, cut:])
 
         def quant_o(c):
             nc.vector.quantize_mx(out=oq[:, cols(c)].bitcast(FP8X4), scales=os_[:, cols(c)], in_=o_bf[c][:].rearrange("p n t -> p (n t)"))
             if c % 2 == 1:
                 both = slice((c - 1) * CHUNK, (c + 1) * CHUNK)
-                nc.scalar.dma_start(out=out_words[:, both], in_=oq[:, both].bitcast(I32))
+                eng = nc.scalar if c == CHUNKS - 1 else nc.sync
+                eng.dma_start(out=out_words[:, both], in_=oq[:, both].bitcast(I32))
 
         quant_w1(0)
         gather(0)
         quant_w1(1)
         first(0)
         for c in range(1, CHUNKS):
-            if c == CHUNKS - 1:
-                deal_scales()
             gather(c)
             first(c)
-        for group in ((round_h, quant_h, second), (gate, product), (round_o, quant_o)):
+        deal_scales()
+        for group in ((round_h, quant_h, second), (gate, product), (round_o,), (quant_o,)):
             for c in range(CHUNKS):
                 for step in group:
                     step(c)

@@ -12,7 +12,6 @@ FP8X4 = mybir.dt.float8_e4m3fn_x4
 FP4X4 = mybir.dt.float4_e2m1fn_x4
 SIGMOID = mybir.ActivationFunctionType.Sigmoid
 MULT = mybir.AluOpType.mult
-ADD = mybir.AluOpType.add
 
 P = 128
 PACK = 4
@@ -161,12 +160,9 @@ def tile_picked_zgrn_lin_po_kernel(tc, x_words, x_scales, w1, w2_words, w2_scale
             src = o32[c][:].rearrange("p t (n i) -> p n t i", i=4)
             cut = CHUNK // 8
             if c < 2:
-                n = CHUNK if c == 0 else CHUNK // 2
-                nc.gpsimd.tensor_scalar(out=o_bf[c][:, 0:n], in0=o32[c][:].rearrange("p t n -> p n t")[:, 0:n], scalar1=1.0, scalar2=0.0, op0=MULT, op1=ADD)
-                if c == 1:
-                    nc.scalar.copy(out=dst[:, cut:], in_=src[:, cut:])
-            elif c == 2:
                 nc.scalar.copy(out=dst, in_=src)
+            elif c == 2:
+                nc.vector.tensor_copy(out=dst, in_=src)
             else:
                 nc.scalar.copy(out=dst[:, 0:cut], in_=src[:, 0:cut])
                 nc.vector.tensor_copy(out=dst[:, cut:], in_=src[:, cut:])

@@ -171,17 +171,17 @@ def tile_picked_zgrn_lin_po_kernel(tc, x_words, x_scales, w1, w2_words, w2_scale
             nc.vector.quantize_mx(out=oq[:, cols(c)].bitcast(FP8X4), scales=os_[:, cols(c)], in_=o_bf[c][:].rearrange("p n t -> p (n t)"))
             if c % 2 == 1:
                 both = slice((c - 1) * CHUNK, (c + 1) * CHUNK)
-                eng = nc.scalar if c == CHUNKS - 1 else nc.sync
-                eng.dma_start(out=out_words[:, both], in_=oq[:, both].bitcast(I32))
+                nc.scalar.dma_start(out=out_words[:, both], in_=oq[:, both].bitcast(I32))
 
         quant_w1(0)
         gather(0)
         quant_w1(1)
         first(0)
         for c in range(1, CHUNKS):
+            if c == CHUNKS - 1:
+                deal_scales()
             gather(c)
             first(c)
-        deal_scales()
         for group in ((round_h, quant_h, second), (gate, product), (round_o,), (quant_o,)):
             for c in range(CHUNKS):
                 for step in group:

@@ -19,7 +19,8 @@ K, T, S, H = 512, 1024, 512, 512
 CHUNK = 128
 CHUNKS = S // CHUNK
 WARM_M = 32
-WARM_PASSES = 12
+WARM_N = 512
+WARM_PASSES = 3
 FLOPS = 2 * K * H * S + 2 * H * H * S
 
 
@@ -61,15 +62,15 @@ def tile_picked_zgrn_lin_po_kernel(tc, x_words, x_scales, w1, w2_words, w2_scale
         nc.vector.tensor_copy(xs[:, 0:CHUNK], xs_win[:].indirect(offsets[:, 0 : CHUNK // 16]))
         nc.vector.tensor_copy(xs[:, CHUNK:S], xs_win[:].indirect(offsets[:, CHUNK // 16 : S // 16]))
 
-        ones = keep.tile([P, CHUNK * PACK], BF16, name="ones", align_bytes=64)
-        nc.vector.memset(ones[:], 1.0)
-        ones_q = keep.tile([P, CHUNK], U32, name="ones_q", align_bytes=64)
-        ones_s = keep.tile([P, CHUNK], U8, name="ones_s", align_bytes=64)
+        ones = keep.tile([P, WARM_N * PACK], BF16, name="ones", align_bytes=64)
+        nc.vector.memset(ones[:].bitcast(I32), 0)
+        ones_q = keep.tile([P, WARM_N], U32, name="ones_q", align_bytes=64)
+        ones_s = keep.tile([P, WARM_N], U8, name="ones_s", align_bytes=64)
         nc.vector.quantize_mx(out=ones_q[:].bitcast(FP8X4), scales=ones_s[:], in_=ones[:])
-        warm_bank = psum.tile([WARM_M, CHUNK], F32, name="warm_bank", tag="zb1_0")
+        warm_bank = psum.tile([WARM_M, WARM_N], F32, name="warm_bank", tag="zb1_2")
         for n_pass in range(WARM_PASSES):
-            nc.tensor.matmul_mx(out=warm_bank[:], lhsT=ones_q[:, 0:WARM_M].bitcast(FP8X4), lhsT_scale=ones_s[:, 0:WARM_M],
-                                rhs=ones_q[:].bitcast(FP8X4), rhs_scale=xs[:, 0:CHUNK], start=True, stop=True)
+            nc.tensor.matmul_mx(out=warm_bank[:], lhsT=ones_q[:, 0:WARM_M].bitcast(FP8X4), lhsT_scale=xs[:, 0:WARM_M],
+                                rhs=ones_q[:].bitcast(FP8X4), rhs_scale=ones_s[:], start=True, stop=True)
 
         w2w = keep.tile([P, 2 * H], U8, name="w2w", align_bytes=64)
         w1_bf = keep.tile([P, H * PACK], BF16, name="w1_bf", align_bytes=64)
@@ -128,36 +129,33 @@ def tile_picked_zgrn_lin_po_kernel(tc, x_words, x_scales, w1, w2_words, w2_scale
             hs[c] = reuse.tile([P, CHUNK], U8, name="hs%d" % c, align_bytes=64, offset=c * CHUNK)
             nc.vector.quantize_mx(out=hq[c][:].bitcast(FP8X4), scales=hs[c][:], in_=h_bf[c][:].rearrange("p n t -> p (n t)"))
 
-        def parts(c):
-            return ((0, 2), (2, 4)) if c == 0 else ((0, 4),)
+        halves = ((0, 2), (2, 4))
+
+        def within(c):
+            return slice((c % 2) * CHUNK, (c % 2 + 1) * CHUNK)
 
         def second(c):
-            for lo, hi in parts(c):
-                zb[c, lo] = psum.tile([P, hi - lo, CHUNK], F32, name="zb%d_%d" % (c, lo), tag="zb%d_%d" % (c % 3, lo))
+            pair = c // 2
+            for lo, hi in halves:
+                if c % 2 == 0:
+                    zb[pair, lo] = psum.tile([P, hi - lo, 2 * CHUNK], F32, name="zb%d_%d" % (pair, lo), tag="zb%d_%d" % (pair, lo))
                 for t in range(lo, hi):
-                    nc.tensor.matmul_mx(out=zb[c, lo][:, t - lo, :], lhsT=w2w[:, 2 * t * P : 2 * (t + 1) * P].bitcast(FP4X4), lhsT_scale=w2s[:, t * P : (t + 1) * P],
+                    nc.tensor.matmul_mx(out=zb[pair, lo][:, t - lo, within(c)], lhsT=w2w[:, 2 * t * P : 2 * (t + 1) * P].bitcast(FP4X4), lhsT_scale=w2s[:, t * P : (t + 1) * P],
                                         rhs=hq[c][:].bitcast(FP8X4), rhs_scale=hs[c][:], start=True, stop=True)
 
-        def spans(c):
-            return (slice(0, CHUNK),) if c == 0 else (slice(0, CHUNK // 2), slice(CHUNK // 2, CHUNK))
-
-        def gate(c):
-            g[c] = keep.tile([P, PACK, CHUNK], F32, name="g%d" % c)
-            for lo, hi in parts(c):
-                for n in spans(c):
-                    nc.scalar.activation(out=g[c][:, lo:hi, n], in_=zb[c, lo][:, :, n], func=SIGMOID)
-
-        def product(c):
-            o32[c] = keep.tile([P, PACK, CHUNK], F32, name="o32_%d" % c)
-            for lo, hi in parts(c):
-                for n in spans(c):
-                    nc.vector.tensor_tensor(out=o32[c][:, lo:hi, n], in0=hb[c][:, lo:hi, n], in1=g[c][:, lo:hi, n], op=MULT)
-                nc.sync.dma_start(out=out_rows[:, lo:hi, cols(c)], in_=o32[c][:, lo:hi, :])
+        def gate_and_product(pair):
+            g[pair] = keep.tile([P, PACK, 2 * CHUNK], F32, name="g%d" % pair)
+            o32[pair] = keep.tile([P, PACK, 2 * CHUNK], F32, name="o32_%d" % pair)
+            for lo, hi in halves:
+                for c in (2 * pair, 2 * pair + 1):
+                    nc.scalar.activation(out=g[pair][:, lo:hi, within(c)], in_=zb[pair, lo][:, :, within(c)], func=SIGMOID)
+                    nc.vector.tensor_tensor(out=o32[pair][:, lo:hi, within(c)], in0=hb[c][:, lo:hi, :], in1=g[pair][:, lo:hi, within(c)], op=MULT)
+                nc.sync.dma_start(out=out_rows[:, lo:hi, pair * 2 * CHUNK : (pair + 1) * 2 * CHUNK], in_=o32[pair][:, lo:hi, :])
 
         def round_o(c):
             o_bf[c] = keep.tile([P, CHUNK, PACK], BF16, name="o_bf%d" % c, align_bytes=64)
             dst = o_bf[c][:].rearrange("p (n i) t -> p n t i", i=4)
-            src = o32[c][:].rearrange("p t (n i) -> p n t i", i=4)
+            src = o32[c // 2][:, :, within(c)].rearrange("p t (n i) -> p n t i", i=4)
             cut = CHUNK // 8
             if c < 2:
                 nc.scalar.copy(out=dst, in_=src)
@@ -182,10 +180,15 @@ def tile_picked_zgrn_lin_po_kernel(tc, x_words, x_scales, w1, w2_words, w2_scale
                 deal_scales()
             gather(c)
             first(c)
-        for group in ((round_h, quant_h, second), (gate, product), (round_o,), (quant_o,)):
+        for c in range(CHUNKS):
+            round_h(c)
+            quant_h(c)
+            second(c)
+        for pair in range(CHUNKS // 2):
+            gate_and_product(pair)
+        for step in (round_o, quant_o):
             for c in range(CHUNKS):
-                for step in group:
-                    step(c)
+                step(c)
         scale_rows = out_2[0].bitcast(I32)
         for q in range(4):
             eng = nc.sync if q < 3 else nc.scalar

@@ -18,6 +18,9 @@ PACK = 4
 K, T, S, H = 512, 1024, 512, 512
 CHUNK = 128
 CHUNKS = S // CHUNK
+W1_FIRST = 224
+W1_PIECES = ((0, W1_FIRST), (W1_FIRST, H))
+CAST_EXTRA = 16
 WARM_M = 32
 WARM_N = 512
 WARM_PASSES = 3
@@ -41,11 +44,11 @@ def tile_picked_zgrn_lin_po_kernel(tc, x_words, x_scales, w1, w2_words, w2_scale
         offsets = keep.tile([P, S // 16], U16, name="offsets")
         w1_rows = w1.rearrange("(p j) c -> p j c", j=PACK)
         w1_raw = []
-        for h in range(2):
-            raw = keep.tile([P, PACK, H // 2], F32, name="w1_raw%d" % h)
-            nc.sync.dma_start(out=raw[:], in_=w1_rows[:, :, h * (H // 2) : (h + 1) * (H // 2)])
+        for n, (lo, hi) in enumerate(W1_PIECES):
+            raw = keep.tile([P, PACK, hi - lo], F32, name="w1_raw%d" % n)
+            nc.sync.dma_start(out=raw[:], in_=w1_rows[:, :, lo:hi])
             w1_raw.append(raw)
-            if h == 0:
+            if n == 0:
                 nc.sync.dma_start(offsets[:], offs)
                 for q in range(4):
                     nc.sync.dma_start(out=xs_win[32 * q : 32 * q + 4, :].bitcast(I32), in_=x_scales[0, 4 * q : 4 * q + 4, :].bitcast(I32))
@@ -67,7 +70,7 @@ def tile_picked_zgrn_lin_po_kernel(tc, x_words, x_scales, w1, w2_words, w2_scale
         ones_q = keep.tile([P, WARM_N], U32, name="ones_q", align_bytes=64)
         ones_s = keep.tile([P, WARM_N], U8, name="ones_s", align_bytes=64)
         nc.vector.quantize_mx(out=ones_q[:].bitcast(FP8X4), scales=ones_s[:], in_=ones[:])
-        warm_bank = psum.tile([WARM_M, WARM_N], F32, name="warm_bank", tag="zb1_2")
+        warm_bank = psum.tile([WARM_M, WARM_N], F32, name="warm_bank", tag="zb1_0")
         for n_pass in range(WARM_PASSES):
             nc.tensor.matmul_mx(out=warm_bank[:], lhsT=ones_q[:, 0:WARM_M].bitcast(FP8X4), lhsT_scale=xs[:, 0:WARM_M],
                                 rhs=ones_q[:].bitcast(FP8X4), rhs_scale=ones_s[:], start=True, stop=True)
@@ -75,11 +78,13 @@ def tile_picked_zgrn_lin_po_kernel(tc, x_words, x_scales, w1, w2_words, w2_scale
         w2w = keep.tile([P, 2 * H], U8, name="w2w", align_bytes=64)
         w1_bf = keep.tile([P, H * PACK], BF16, name="w1_bf", align_bytes=64)
         w1_dealt = w1_bf[:].rearrange("p (t m j) -> p m j t", t=PACK, j=PACK)
-        half = P // 2
-        nc.scalar.copy(out=w1_dealt[:, 0:half], in_=w1_raw[0][:].rearrange("p j (m t) -> p m j t", t=PACK))
-        second_half = w1_raw[1][:].rearrange("p j (m t) -> p m j t", t=PACK)
-        nc.scalar.copy(out=w1_dealt[:, half:P, :, 0:2], in_=second_half[:, :, :, 0:2])
-        nc.scalar.copy(out=w1_dealt[:, half:P, :, 2:4], in_=second_half[:, :, :, 2:4])
+        src = [r[:].rearrange("p j (m t) -> p m j t", t=PACK) for r in w1_raw]
+        first_m = W1_FIRST // PACK
+        rest = w1_dealt[:, first_m:P]
+        nc.scalar.copy(out=w1_dealt[:, 0:first_m], in_=src[0])
+        nc.vector.tensor_copy(out=rest[:, :, :, 0:2], in_=src[1][:, :, :, 0:2])
+        nc.vector.tensor_copy(out=rest[:, 0:CAST_EXTRA, :, 2:4], in_=src[1][:, 0:CAST_EXTRA, :, 2:4])
+        nc.scalar.copy(out=rest[:, CAST_EXTRA:, :, 2:4], in_=src[1][:, CAST_EXTRA:, :, 2:4])
         w2s = keep.tile([P, H], U8, name="w2s", align_bytes=64)
 
         def deal_scales():
@@ -120,7 +125,7 @@ def tile_picked_zgrn_lin_po_kernel(tc, x_words, x_scales, w1, w2_words, w2_scale
                                     rhs=xw[c][:].bitcast(FP8X4), rhs_scale=xs[:, cols(c)], start=True, stop=True)
 
         def round_h(c):
-            h_bf[c] = keep.tile([P, CHUNK, PACK], BF16, name="h_bf%d" % c, tag="h_bf", bufs=2, align_bytes=64)
+            h_bf[c] = keep.tile([P, CHUNK, PACK], BF16, name="h_bf%d" % c, tag="h_bf%d" % (c % 3), align_bytes=64)
             copy = nc.vector.tensor_copy if c == CHUNKS - 1 else nc.scalar.copy
             copy(out=h_bf[c][:], in_=hb[c][:].rearrange("p t n -> p n t"))
 
@@ -135,22 +140,27 @@ def tile_picked_zgrn_lin_po_kernel(tc, x_words, x_scales, w1, w2_words, w2_scale
             return slice((c % 2) * CHUNK, (c % 2 + 1) * CHUNK)
 
         def second(c):
-            pair = c // 2
-            for lo, hi in halves:
-                if c % 2 == 0:
-                    zb[pair, lo] = psum.tile([P, hi - lo, 2 * CHUNK], F32, name="zb%d_%d" % (pair, lo), tag="zb%d_%d" % (pair, lo))
+            for lo, hi in halves if c == 0 else ((0, PACK),):
+                bank = psum.tile([P, hi - lo, CHUNK], F32, name="zb%d_%d" % (c, lo), tag="zb%d_%d" % (c % 3, lo))
                 for t in range(lo, hi):
-                    nc.tensor.matmul_mx(out=zb[pair, lo][:, t - lo, within(c)], lhsT=w2w[:, 2 * t * P : 2 * (t + 1) * P].bitcast(FP4X4), lhsT_scale=w2s[:, t * P : (t + 1) * P],
+                    nc.tensor.matmul_mx(out=bank[:, t - lo, :], lhsT=w2w[:, 2 * t * P : 2 * (t + 1) * P].bitcast(FP4X4), lhsT_scale=w2s[:, t * P : (t + 1) * P],
                                         rhs=hq[c][:].bitcast(FP8X4), rhs_scale=hs[c][:], start=True, stop=True)
+                for a, b in halves:
+                    if lo <= a and b <= hi:
+                        zb[c, a] = bank[:, a - lo : b - lo, :]
 
         def gate_and_product(pair):
             g[pair] = keep.tile([P, PACK, 2 * CHUNK], F32, name="g%d" % pair)
             o32[pair] = keep.tile([P, PACK, 2 * CHUNK], F32, name="o32_%d" % pair)
-            for lo, hi in halves:
-                for c in (2 * pair, 2 * pair + 1):
-                    nc.scalar.activation(out=g[pair][:, lo:hi, within(c)], in_=zb[pair, lo][:, :, within(c)], func=SIGMOID)
-                    nc.vector.tensor_tensor(out=o32[pair][:, lo:hi, within(c)], in0=hb[c][:, lo:hi, :], in1=g[pair][:, lo:hi, within(c)], op=MULT)
-                nc.sync.dma_start(out=out_rows[:, lo:hi, pair * 2 * CHUNK : (pair + 1) * 2 * CHUNK], in_=o32[pair][:, lo:hi, :])
+            both = (2 * pair, 2 * pair + 1)
+            steps = [(c, h) for c in both for h in halves] if pair == 0 else [(c, h) for h in halves for c in both]
+            for c, (lo, hi) in steps:
+                nc.scalar.activation(out=g[pair][:, lo:hi, within(c)], in_=zb[c, lo], func=SIGMOID)
+                nc.vector.tensor_tensor(out=o32[pair][:, lo:hi, within(c)], in0=hb[c][:, lo:hi, :], in1=g[pair][:, lo:hi, within(c)], op=MULT)
+                if pair == 0 and hi == PACK:
+                    nc.sync.dma_start(out=out_rows[:, :, cols(c)], in_=o32[pair][:, :, within(c)])
+                if pair == 1 and c % 2 == 1:
+                    nc.sync.dma_start(out=out_rows[:, lo:hi, pair * 2 * CHUNK : (pair + 1) * 2 * CHUNK], in_=o32[pair][:, lo:hi, :])
 
         def round_o(c):
             o_bf[c] = keep.tile([P, CHUNK, PACK], BF16, name="o_bf%d" % c, align_bytes=64)
@@ -172,18 +182,21 @@ def tile_picked_zgrn_lin_po_kernel(tc, x_words, x_scales, w1, w2_words, w2_scale
                 nc.scalar.dma_start(out=out_words[:, both], in_=oq[:, both].bitcast(I32))
 
         quant_w1(0)
-        gather(0)
         quant_w1(1)
+        gather(0)
         first(0)
         for c in range(1, CHUNKS):
             if c == CHUNKS - 1:
                 deal_scales()
             gather(c)
             first(c)
-        for c in range(CHUNKS):
-            round_h(c)
-            quant_h(c)
-            second(c)
+        for pair in range(CHUNKS // 2):
+            both = (2 * pair, 2 * pair + 1)
+            for c in both:
+                round_h(c)
+            for c in both:
+                quant_h(c)
+                second(c)
         for pair in range(CHUNKS // 2):
             gate_and_product(pair)
         for step in (round_o, quant_o):

@@ -125,13 +125,23 @@ def tile_picked_zgrn_lin_po_kernel(tc, x_words, x_scales, w1, w2_words, w2_scale
                                     rhs=xw[c][:].bitcast(FP8X4), rhs_scale=xs[:, cols(c)], start=True, stop=True)
 
         def round_h(c):
-            h_bf[c] = keep.tile([P, CHUNK, PACK], BF16, name="h_bf%d" % c, tag="h_bf%d" % (c % 3), align_bytes=64)
-            copy = nc.vector.tensor_copy if c == CHUNKS - 1 else nc.scalar.copy
-            copy(out=h_bf[c][:], in_=hb[c][:].rearrange("p t n -> p n t"))
+            if c == CHUNKS - 1:
+                h_bf[c] = reuse.tile([P, CHUNK, PACK], BF16, name="h_bf%d" % c, align_bytes=64, offset=c * CHUNK)
+            else:
+                h_bf[c] = keep.tile([P, CHUNK, PACK], BF16, name="h_bf%d" % c, align_bytes=64)
+            if c < CHUNKS - 1:
+                nc.scalar.copy(out=h_bf[c][:], in_=hb[c][:].rearrange("p t n -> p n t"))
+
+        def round_last(u):
+            part = slice(u * CHUNK // 2, (u + 1) * CHUNK // 2)
+            nc.vector.tensor_copy(out=h_bf[CHUNKS - 1][:, part], in_=hb[CHUNKS - 1][:].rearrange("p t n -> p n t")[:, part])
 
         def quant_h(c):
             hq[c] = keep.tile([P, CHUNK], U32, name="hq%d" % c, align_bytes=64)
-            hs[c] = reuse.tile([P, CHUNK], U8, name="hs%d" % c, align_bytes=64, offset=c * CHUNK)
+            if c == CHUNKS - 1:
+                hs[c] = keep.tile([P, CHUNK], U8, name="hs%d" % c, align_bytes=64)
+            else:
+                hs[c] = reuse.tile([P, CHUNK], U8, name="hs%d" % c, align_bytes=64, offset=c * CHUNK)
             nc.vector.quantize_mx(out=hq[c][:].bitcast(FP8X4), scales=hs[c][:], in_=h_bf[c][:].rearrange("p n t -> p (n t)"))
 
         halves = ((0, 2), (2, 4))
@@ -166,14 +176,10 @@ def tile_picked_zgrn_lin_po_kernel(tc, x_words, x_scales, w1, w2_words, w2_scale
             o_bf[c] = keep.tile([P, CHUNK, PACK], BF16, name="o_bf%d" % c, align_bytes=64)
             dst = o_bf[c][:].rearrange("p (n i) t -> p n t i", i=4)
             src = o32[c // 2][:, :, within(c)].rearrange("p t (n i) -> p n t i", i=4)
-            cut = CHUNK // 8
-            if c < 2:
+            if c % 2 == 0:
                 nc.scalar.copy(out=dst, in_=src)
-            elif c == 2:
-                nc.vector.tensor_copy(out=dst, in_=src)
             else:
-                nc.scalar.copy(out=dst[:, 0:cut], in_=src[:, 0:cut])
-                nc.vector.tensor_copy(out=dst[:, cut:], in_=src[:, cut:])
+                nc.vector.tensor_copy(out=dst, in_=src)
 
         def quant_o(c):
             nc.vector.quantize_mx(out=oq[:, cols(c)].bitcast(FP8X4), scales=os_[:, cols(c)], in_=o_bf[c][:].rearrange("p n t -> p (n t)"))
@@ -190,18 +196,19 @@ def tile_picked_zgrn_lin_po_kernel(tc, x_words, x_scales, w1, w2_words, w2_scale
                 deal_scales()
             gather(c)
             first(c)
-        for pair in range(CHUNKS // 2):
-            both = (2 * pair, 2 * pair + 1)
-            for c in both:
-                round_h(c)
-            for c in both:
-                quant_h(c)
-                second(c)
+        for c in range(CHUNKS):
+            round_h(c)
+        for c in range(CHUNKS):
+            quant_h(c)
+            second(c)
+            if c < 2:
+                round_last(c)
         for pair in range(CHUNKS // 2):
             gate_and_product(pair)
-        for step in (round_o, quant_o):
-            for c in range(CHUNKS):
-                step(c)
+        for c in range(CHUNKS):
+            round_o(c)
+        for c in range(CHUNKS):
+            quant_o(c)
         scale_rows = out_2[0].bitcast(I32)
         for q in range(4):
             eng = nc.sync if q < 3 else nc.scalar

@@ -21,6 +21,7 @@ CHUNKS = S // CHUNK
 W1_FIRST = 224
 W1_PIECES = ((0, W1_FIRST), (W1_FIRST, H))
 CAST_EXTRA = 16
+DMA_ALIGN = 256
 WARM_M = 32
 WARM_N = 512
 WARM_PASSES = 3
@@ -34,29 +35,29 @@ def tile_picked_zgrn_lin_po_kernel(tc, x_words, x_scales, w1, w2_words, w2_scale
         reuse = ctx.enter_context(tc.tile_pool(name="reuse", bufs=1))
         psum = ctx.enter_context(tc.psum_pool(name="psum", bufs=1))
 
-        xs_win = keep.tile([P, T], U8, name="xs_win", align_bytes=64)
+        xs_win = keep.tile([P, T], U8, name="xs_win", align_bytes=DMA_ALIGN)
         nc.vector.memset(xs_win[:].bitcast(I32), 0)
         warm_in = keep.tile([P, 8], F32, name="warm_in")
         warm_out = keep.tile([P, 8], F32, name="warm_out")
         nc.vector.memset(warm_in[:], 0.0)
         nc.scalar.activation(out=warm_out[:], in_=warm_in[:], func=SIGMOID)
 
-        offsets = keep.tile([P, S // 16], U16, name="offsets")
+        offsets = keep.tile([P, S // 16], U16, name="offsets", align_bytes=DMA_ALIGN)
         w1_rows = w1.rearrange("(p j) c -> p j c", j=PACK)
         w1_raw = []
         for n, (lo, hi) in enumerate(W1_PIECES):
-            raw = keep.tile([P, PACK, hi - lo], F32, name="w1_raw%d" % n)
+            raw = keep.tile([P, PACK, hi - lo], F32, name="w1_raw%d" % n, align_bytes=DMA_ALIGN)
             nc.sync.dma_start(out=raw[:], in_=w1_rows[:, :, lo:hi])
             w1_raw.append(raw)
             if n == 0:
                 nc.sync.dma_start(offsets[:], offs)
                 for q in range(4):
                     nc.sync.dma_start(out=xs_win[32 * q : 32 * q + 4, :].bitcast(I32), in_=x_scales[0, 4 * q : 4 * q + 4, :].bitcast(I32))
-        xw_win = keep.tile([P, T], I32, name="xw_win", align_bytes=64)
+        xw_win = keep.tile([P, T], I32, name="xw_win", align_bytes=DMA_ALIGN)
         nc.sync.dma_start(out=xw_win[:], in_=x_words[0].rearrange("p c r -> p (c r)").bitcast(I32))
-        w2w_raw = keep.tile([P, 2 * H], U8, name="w2w_raw", align_bytes=64)
+        w2w_raw = keep.tile([P, 2 * H], U8, name="w2w_raw", align_bytes=DMA_ALIGN)
         nc.sync.dma_start(out=w2w_raw[:].bitcast(I32), in_=w2_words[0].bitcast(I32))
-        w2s_raw = reuse.tile([P, H], U8, name="w2s_raw", align_bytes=64, offset=0)
+        w2s_raw = reuse.tile([P, H], U8, name="w2s_raw", align_bytes=DMA_ALIGN, offset=0)
         nc.vector.memset(w2s_raw[:].bitcast(I32), 0)
         for q in range(4):
             nc.sync.dma_start(out=w2s_raw[32 * q : 32 * q + 4, :].bitcast(I32), in_=w2_scales[0, 4 * q : 4 * q + 4, :].bitcast(I32))
@@ -104,8 +105,8 @@ def tile_picked_zgrn_lin_po_kernel(tc, x_words, x_scales, w1, w2_words, w2_scale
             part = slice(u * 2 * P, (u + 1) * 2 * P)
             nc.vector.quantize_mx(out=w1q[:, part].bitcast(FP8X4), scales=w1s[:, part], in_=w1_bf[:, u * 2 * P * PACK : (u + 1) * 2 * P * PACK])
 
-        oq = keep.tile([P, S], U32, name="oq", align_bytes=64)
-        os_ = keep.tile([P, S], U8, name="os_", align_bytes=64)
+        oq = keep.tile([P, S], U32, name="oq", align_bytes=DMA_ALIGN)
+        os_ = keep.tile([P, S], U8, name="os_", align_bytes=DMA_ALIGN)
         out_rows = out_0.rearrange("(p t) n -> p t n", t=PACK)
         out_words = out_1[0].rearrange("p c r -> p (c r)").bitcast(I32)
 
@@ -161,7 +162,7 @@ def tile_picked_zgrn_lin_po_kernel(tc, x_words, x_scales, w1, w2_words, w2_scale
 
         def gate_and_product(pair):
             g[pair] = keep.tile([P, PACK, 2 * CHUNK], F32, name="g%d" % pair)
-            o32[pair] = keep.tile([P, PACK, 2 * CHUNK], F32, name="o32_%d" % pair)
+            o32[pair] = keep.tile([P, PACK, 2 * CHUNK], F32, name="o32_%d" % pair, align_bytes=DMA_ALIGN)
             both = (2 * pair, 2 * pair + 1)
             steps = [(c, h) for c in both for h in halves] if pair == 0 else [(c, h) for h in halves for c in both]
             for c, (lo, hi) in steps:

@@ -18,7 +18,7 @@ PACK = 4
 K, T, S, H = 512, 1024, 512, 512
 CHUNK = 128
 CHUNKS = S // CHUNK
-W1_FIRST = 224
+W1_FIRST = 256
 W1_PIECES = ((0, W1_FIRST), (W1_FIRST, H))
 CAST_EXTRA = 16
 DMA_ALIGN = 256
@@ -161,7 +161,7 @@ def tile_picked_zgrn_lin_po_kernel(tc, x_words, x_scales, w1, w2_words, w2_scale
                         zb[c, a] = bank[:, a - lo : b - lo, :]
 
         def gate_and_product(pair):
-            g[pair] = keep.tile([P, PACK, 2 * CHUNK], F32, name="g%d" % pair)
+            g[pair] = keep.tile([P, PACK, 2 * CHUNK], F32, name="g%d" % pair, align_bytes=DMA_ALIGN)
             o32[pair] = keep.tile([P, PACK, 2 * CHUNK], F32, name="o32_%d" % pair, align_bytes=DMA_ALIGN)
             both = (2 * pair, 2 * pair + 1)
             steps = [(c, h) for c in both for h in halves] if pair == 0 else [(c, h) for h in halves for c in both]

@@ -18,9 +18,9 @@ PACK = 4
 K, T, S, H = 512, 1024, 512, 512
 CHUNK = 128
 CHUNKS = S // CHUNK
-W1_FIRST = 256
+W1_FIRST = 192
 W1_PIECES = ((0, W1_FIRST), (W1_FIRST, H))
-CAST_EXTRA = 16
+CAST_VECTOR = (52, 44)
 DMA_ALIGN = 256
 WARM_M = 32
 WARM_N = 512
@@ -83,9 +83,9 @@ def tile_picked_zgrn_lin_po_kernel(tc, x_words, x_scales, w1, w2_words, w2_scale
         first_m = W1_FIRST // PACK
         rest = w1_dealt[:, first_m:P]
         nc.scalar.copy(out=w1_dealt[:, 0:first_m], in_=src[0])
-        nc.vector.tensor_copy(out=rest[:, :, :, 0:2], in_=src[1][:, :, :, 0:2])
-        nc.vector.tensor_copy(out=rest[:, 0:CAST_EXTRA, :, 2:4], in_=src[1][:, 0:CAST_EXTRA, :, 2:4])
-        nc.scalar.copy(out=rest[:, CAST_EXTRA:, :, 2:4], in_=src[1][:, CAST_EXTRA:, :, 2:4])
+        for (lo, hi), cut in zip(((0, 2), (2, 4)), CAST_VECTOR):
+            nc.vector.tensor_copy(out=rest[:, 0:cut, :, lo:hi], in_=src[1][:, 0:cut, :, lo:hi])
+            nc.scalar.copy(out=rest[:, cut:, :, lo:hi], in_=src[1][:, cut:, :, lo:hi])
         w2s = keep.tile([P, H], U8, name="w2s", align_bytes=64)
 
         def deal_scales():
@@ -168,7 +168,9 @@ def tile_picked_zgrn_lin_po_kernel(tc, x_words, x_scales, w1, w2_words, w2_scale
             for c, (lo, hi) in steps:
                 nc.scalar.activation(out=g[pair][:, lo:hi, within(c)], in_=zb[c, lo], func=SIGMOID)
                 nc.vector.tensor_tensor(out=o32[pair][:, lo:hi, within(c)], in0=hb[c][:, lo:hi, :], in1=g[pair][:, lo:hi, within(c)], op=MULT)
-                if pair == 0 and hi == PACK:
+                if c == 0:
+                    nc.sync.dma_start(out=out_rows[:, lo:hi, cols(c)], in_=o32[pair][:, lo:hi, within(c)])
+                if c == 1 and hi == PACK:
                     nc.sync.dma_start(out=out_rows[:, :, cols(c)], in_=o32[pair][:, :, within(c)])
                 if pair == 1 and c % 2 == 1:
                     nc.sync.dma_start(out=out_rows[:, lo:hi, pair * 2 * CHUNK : (pair + 1) * 2 * CHUNK], in_=o32[pair][:, lo:hi, :])

@@ -18,200 +18,175 @@ PACK = 4
 K, T, S, H = 512, 1024, 512, 512
 CHUNK = 128
 CHUNKS = S // CHUNK
+HALF = CHUNK // 2
 W1_FIRST = 192
-W1_PIECES = ((0, W1_FIRST), (W1_FIRST, H))
+FIRST_CAST_VECTOR = 18
 CAST_VECTOR = (52, 44)
-DMA_ALIGN = 256
 WARM_M = 32
 WARM_N = 512
 WARM_PASSES = 3
+DMA_ALIGN = 256
 FLOPS = 2 * K * H * S + 2 * H * H * S
+SLICE_PAIRS = ((0, 2), (2, 4))
+GATE_ORDER = ((0, 0), (0, 2), (1, 0), (1, 2), (2, 0), (3, 0), (2, 2), (3, 2))
+GATE_BANKS = 4
 
 
 def tile_picked_zgrn_lin_po_kernel(tc, x_words, x_scales, w1, w2_words, w2_scales, offs, out_0, out_1, out_2):
     nc = tc.nc
     with ExitStack() as ctx:
         keep = ctx.enter_context(tc.tile_pool(name="keep", bufs=1))
-        reuse = ctx.enter_context(tc.tile_pool(name="reuse", bufs=1))
+        after_words = ctx.enter_context(tc.tile_pool(name="after_words", bufs=1))
+        after_scales = ctx.enter_context(tc.tile_pool(name="after_scales", bufs=1))
         psum = ctx.enter_context(tc.psum_pool(name="psum", bufs=1))
 
         xs_win = keep.tile([P, T], U8, name="xs_win", align_bytes=DMA_ALIGN)
         nc.vector.memset(xs_win[:].bitcast(I32), 0)
-        warm_in = keep.tile([P, 8], F32, name="warm_in")
-        warm_out = keep.tile([P, 8], F32, name="warm_out")
-        nc.vector.memset(warm_in[:], 0.0)
-        nc.scalar.activation(out=warm_out[:], in_=warm_in[:], func=SIGMOID)
+        table_in = keep.tile([P, 8], F32, name="table_in")
+        table_out = keep.tile([P, 8], F32, name="table_out")
+        nc.vector.memset(table_in[:], 0.0)
+        nc.scalar.activation(out=table_out[:], in_=table_in[:], func=SIGMOID)
 
         offsets = keep.tile([P, S // 16], U16, name="offsets", align_bytes=DMA_ALIGN)
         w1_rows = w1.rearrange("(p j) c -> p j c", j=PACK)
-        w1_raw = []
-        for n, (lo, hi) in enumerate(W1_PIECES):
-            raw = keep.tile([P, PACK, hi - lo], F32, name="w1_raw%d" % n, align_bytes=DMA_ALIGN)
-            nc.sync.dma_start(out=raw[:], in_=w1_rows[:, :, lo:hi])
-            w1_raw.append(raw)
-            if n == 0:
-                nc.sync.dma_start(offsets[:], offs)
-                for q in range(4):
-                    nc.sync.dma_start(out=xs_win[32 * q : 32 * q + 4, :].bitcast(I32), in_=x_scales[0, 4 * q : 4 * q + 4, :].bitcast(I32))
+        w1_a = keep.tile([P, PACK, W1_FIRST], F32, name="w1_a", align_bytes=DMA_ALIGN)
+        w1_b = keep.tile([P, PACK, H - W1_FIRST], F32, name="w1_b", align_bytes=DMA_ALIGN)
         xw_win = keep.tile([P, T], I32, name="xw_win", align_bytes=DMA_ALIGN)
-        nc.sync.dma_start(out=xw_win[:], in_=x_words[0].rearrange("p c r -> p (c r)").bitcast(I32))
-        w2w_raw = keep.tile([P, 2 * H], U8, name="w2w_raw", align_bytes=DMA_ALIGN)
-        nc.sync.dma_start(out=w2w_raw[:].bitcast(I32), in_=w2_words[0].bitcast(I32))
-        w2s_raw = reuse.tile([P, H], U8, name="w2s_raw", align_bytes=DMA_ALIGN, offset=0)
+        w2w_raw = after_words.tile([P, 2 * H], U8, name="w2w_raw", align_bytes=DMA_ALIGN, offset=1024)
+        w2s_raw = after_scales.tile([P, H], U8, name="w2s_raw", align_bytes=DMA_ALIGN, offset=1024)
         nc.vector.memset(w2s_raw[:].bitcast(I32), 0)
+
+        nc.sync.dma_start(out=w1_a[:], in_=w1_rows[:, :, 0:W1_FIRST])
+        nc.sync.dma_start(offsets[:], offs)
+        for q in range(4):
+            nc.sync.dma_start(out=xs_win[32 * q : 32 * q + 4, :].bitcast(I32), in_=x_scales[0, 4 * q : 4 * q + 4, :].bitcast(I32))
+        nc.sync.dma_start(out=w1_b[:], in_=w1_rows[:, :, W1_FIRST:H])
+        nc.sync.dma_start(out=xw_win[:], in_=x_words[0].rearrange("p c r -> p (c r)").bitcast(I32))
+        nc.sync.dma_start(out=w2w_raw[:].bitcast(I32), in_=w2_words[0].bitcast(I32))
         for q in range(4):
             nc.sync.dma_start(out=w2s_raw[32 * q : 32 * q + 4, :].bitcast(I32), in_=w2_scales[0, 4 * q : 4 * q + 4, :].bitcast(I32))
 
-        xs = keep.tile([P, S], U8, name="xs", align_bytes=64)
-        nc.vector.tensor_copy(xs[:, 0:CHUNK], xs_win[:].indirect(offsets[:, 0 : CHUNK // 16]))
-        nc.vector.tensor_copy(xs[:, CHUNK:S], xs_win[:].indirect(offsets[:, CHUNK // 16 : S // 16]))
-
-        ones = keep.tile([P, WARM_N * PACK], BF16, name="ones", align_bytes=64)
-        nc.vector.memset(ones[:].bitcast(I32), 0)
-        ones_q = keep.tile([P, WARM_N], U32, name="ones_q", align_bytes=64)
-        ones_s = keep.tile([P, WARM_N], U8, name="ones_s", align_bytes=64)
-        nc.vector.quantize_mx(out=ones_q[:].bitcast(FP8X4), scales=ones_s[:], in_=ones[:])
-        warm_bank = psum.tile([WARM_M, WARM_N], F32, name="warm_bank", tag="zb1_0")
-        for n_pass in range(WARM_PASSES):
-            nc.tensor.matmul_mx(out=warm_bank[:], lhsT=ones_q[:, 0:WARM_M].bitcast(FP8X4), lhsT_scale=xs[:, 0:WARM_M],
-                                rhs=ones_q[:].bitcast(FP8X4), rhs_scale=ones_s[:], start=True, stop=True)
-
-        w2w = keep.tile([P, 2 * H], U8, name="w2w", align_bytes=64)
         w1_bf = keep.tile([P, H * PACK], BF16, name="w1_bf", align_bytes=64)
         w1_dealt = w1_bf[:].rearrange("p (t m j) -> p m j t", t=PACK, j=PACK)
-        src = [r[:].rearrange("p j (m t) -> p m j t", t=PACK) for r in w1_raw]
-        first_m = W1_FIRST // PACK
-        rest = w1_dealt[:, first_m:P]
-        nc.scalar.copy(out=w1_dealt[:, 0:first_m], in_=src[0])
-        for (lo, hi), cut in zip(((0, 2), (2, 4)), CAST_VECTOR):
-            nc.vector.tensor_copy(out=rest[:, 0:cut, :, lo:hi], in_=src[1][:, 0:cut, :, lo:hi])
-            nc.scalar.copy(out=rest[:, cut:, :, lo:hi], in_=src[1][:, cut:, :, lo:hi])
-        w2s = keep.tile([P, H], U8, name="w2s", align_bytes=64)
-
-        def deal_scales():
-            nc.vector.tensor_copy(
-                out=w2w[:].bitcast(U16).rearrange("p (t m) -> p t m", t=PACK),
-                in_=w2w_raw[:].bitcast(U16).rearrange("p (m t) -> p t m", t=PACK),
-            )
-            nc.vector.tensor_copy(
-                out=w2s[:].rearrange("p (t m) -> p t m", t=PACK),
-                in_=w2s_raw[:].rearrange("p (m t) -> p t m", t=PACK),
-            )
-
+        src_a = w1_a[:].rearrange("p j (m t) -> p m j t", t=PACK)
+        src_b = w1_b[:].rearrange("p j (m t) -> p m j t", t=PACK)
+        rest = w1_dealt[:, W1_FIRST // PACK : P]
+        warm_bf = keep.tile([P, WARM_M * PACK], BF16, name="warm_bf", align_bytes=64)
+        nc.vector.tensor_copy(out=warm_bf[:], in_=w1_a[:, 0, 0 : WARM_M * PACK])
+        nc.vector.tensor_copy(out=w1_dealt[:, 0:FIRST_CAST_VECTOR], in_=src_a[:, 0:FIRST_CAST_VECTOR])
+        nc.scalar.copy(out=w1_dealt[:, FIRST_CAST_VECTOR : W1_FIRST // PACK], in_=src_a[:, FIRST_CAST_VECTOR:])
+        warm_q = keep.tile([P, WARM_M], U32, name="warm_q", align_bytes=64)
+        warm_s = keep.tile([P, WARM_M], U8, name="warm_s", align_bytes=64)
+        nc.vector.memset(warm_s[:].bitcast(I32), 0)
+        nc.vector.quantize_mx(out=warm_q[:].bitcast(FP8X4), scales=warm_s[:], in_=warm_bf[:])
+        wide_q = keep.tile([P, WARM_N], U32, name="wide_q", align_bytes=64)
+        wide_s = keep.tile([P, WARM_N], U8, name="wide_s", align_bytes=64)
+        reps = WARM_N // WARM_M
+        nc.scalar.copy(out=wide_q[:].rearrange("p (r m) -> p r m", r=reps), in_=warm_q[:].unsqueeze(1).to_broadcast([P, reps, WARM_M]))
+        nc.scalar.copy(out=wide_s[:].bitcast(U32).rearrange("p (r m) -> p r m", r=reps), in_=warm_s[:].bitcast(U32).unsqueeze(1).to_broadcast([P, reps, WARM_M // 4]))
+        warm_bank = psum.tile([WARM_M, WARM_N], F32, name="warm_bank", tag="z3")
+        for n_pass in range(WARM_PASSES):
+            nc.tensor.matmul_mx(out=warm_bank[:], lhsT=warm_q[:].bitcast(FP8X4), lhsT_scale=warm_s[:],
+                                rhs=wide_q[:].bitcast(FP8X4), rhs_scale=wide_s[:], start=True, stop=True)
+        xs = keep.tile([P, S], U8, name="xs", align_bytes=64)
+        nc.vector.tensor_copy(xs[:], xs_win[:].indirect(offsets[:]))
+        for (lo, hi), cut in zip(SLICE_PAIRS, CAST_VECTOR):
+            nc.vector.tensor_copy(out=rest[:, 0:cut, :, lo:hi], in_=src_b[:, 0:cut, :, lo:hi])
+            nc.scalar.copy(out=rest[:, cut:, :, lo:hi], in_=src_b[:, cut:, :, lo:hi])
         w1q = keep.tile([P, H], U32, name="w1q", align_bytes=64)
         w1s = keep.tile([P, H], U8, name="w1s", align_bytes=64)
-
-        def quant_w1(u):
-            part = slice(u * 2 * P, (u + 1) * 2 * P)
-            nc.vector.quantize_mx(out=w1q[:, part].bitcast(FP8X4), scales=w1s[:, part], in_=w1_bf[:, u * 2 * P * PACK : (u + 1) * 2 * P * PACK])
-
-        oq = keep.tile([P, S], U32, name="oq", align_bytes=DMA_ALIGN)
-        os_ = keep.tile([P, S], U8, name="os_", align_bytes=DMA_ALIGN)
-        out_rows = out_0.rearrange("(p t) n -> p t n", t=PACK)
-        out_words = out_1[0].rearrange("p c r -> p (c r)").bitcast(I32)
-
-        xw, hb, zb, h_bf, hq, hs, g, o32, o_bf = {}, {}, {}, {}, {}, {}, {}, {}, {}
+        for lo, hi in SLICE_PAIRS:
+            nc.vector.quantize_mx(out=w1q[:, lo * P : hi * P].bitcast(FP8X4), scales=w1s[:, lo * P : hi * P], in_=w1_bf[:, lo * P * PACK : hi * P * PACK])
 
         def cols(c):
             return slice(c * CHUNK, (c + 1) * CHUNK)
 
-        def gather(c):
-            xw[c] = keep.tile([P, CHUNK], U32, name="xw%d" % c, align_bytes=64)
-            nc.vector.tensor_copy(xw[c][:], xw_win[:].bitcast(U32).indirect(offsets[:, c * 8 : (c + 1) * 8]))
-
-        def first(c):
-            hb[c] = psum.tile([P, PACK, CHUNK], F32, name="hb%d" % c)
+        h_bank = []
+        for c in range(CHUNKS):
+            if c == CHUNKS - 1:
+                xw = after_words.tile([P, CHUNK], U32, name="xw%d" % c, align_bytes=64, offset=2560)
+            else:
+                xw = keep.tile([P, CHUNK], U32, name="xw%d" % c, align_bytes=64)
+            nc.vector.tensor_copy(xw[:], xw_win[:].bitcast(U32).indirect(offsets[:, c * 8 : (c + 1) * 8]))
+            bank = psum.tile([P, PACK, CHUNK], F32, name="h_bank%d" % c)
             for t in range(PACK):
-                nc.tensor.matmul_mx(out=hb[c][:, t, :], lhsT=w1q[:, t * P : (t + 1) * P].bitcast(FP8X4), lhsT_scale=w1s[:, t * P : (t + 1) * P],
-                                    rhs=xw[c][:].bitcast(FP8X4), rhs_scale=xs[:, cols(c)], start=True, stop=True)
+                nc.tensor.matmul_mx(out=bank[:, t, :], lhsT=w1q[:, t * P : (t + 1) * P].bitcast(FP8X4), lhsT_scale=w1s[:, t * P : (t + 1) * P],
+                                    rhs=xw[:].bitcast(FP8X4), rhs_scale=xs[:, cols(c)], start=True, stop=True)
+            h_bank.append(bank)
 
-        def round_h(c):
-            if c == CHUNKS - 1:
-                h_bf[c] = reuse.tile([P, CHUNK, PACK], BF16, name="h_bf%d" % c, align_bytes=64, offset=c * CHUNK)
-            else:
-                h_bf[c] = keep.tile([P, CHUNK, PACK], BF16, name="h_bf%d" % c, align_bytes=64)
-            if c < CHUNKS - 1:
-                nc.scalar.copy(out=h_bf[c][:], in_=hb[c][:].rearrange("p t n -> p n t"))
+        w2w = keep.tile([P, 2 * H], U8, name="w2w", align_bytes=64)
+        w2s = keep.tile([P, H], U8, name="w2s", align_bytes=64)
+        nc.scalar.copy(out=w2w[:].bitcast(U16).rearrange("p (t m) -> p t m", t=PACK), in_=w2w_raw[:].bitcast(U16).rearrange("p (m t) -> p t m", t=PACK))
+        nc.vector.tensor_copy(out=w2s[:].rearrange("p (t m) -> p t m", t=PACK), in_=w2s_raw[:].rearrange("p (m t) -> p t m", t=PACK))
 
-        def round_last(u):
-            part = slice(u * CHUNK // 2, (u + 1) * CHUNK // 2)
-            nc.vector.tensor_copy(out=h_bf[CHUNKS - 1][:, part], in_=hb[CHUNKS - 1][:].rearrange("p t n -> p n t")[:, part])
-
-        def quant_h(c):
-            hq[c] = keep.tile([P, CHUNK], U32, name="hq%d" % c, align_bytes=64)
-            if c == CHUNKS - 1:
-                hs[c] = keep.tile([P, CHUNK], U8, name="hs%d" % c, align_bytes=64)
-            else:
-                hs[c] = reuse.tile([P, CHUNK], U8, name="hs%d" % c, align_bytes=64, offset=c * CHUNK)
-            nc.vector.quantize_mx(out=hq[c][:].bitcast(FP8X4), scales=hs[c][:], in_=h_bf[c][:].rearrange("p n t -> p (n t)"))
-
-        halves = ((0, 2), (2, 4))
+        h_bf = [
+            after_words.tile([P, CHUNK, PACK], BF16, name="h_bf0", align_bytes=64, offset=512),
+            after_words.tile([P, CHUNK, PACK], BF16, name="h_bf1", align_bytes=64, offset=1536),
+            after_words.tile([P, CHUNK, PACK], BF16, name="h_bf2", align_bytes=64, offset=2560),
+            after_scales.tile([P, CHUNK, PACK], BF16, name="h_bf3", align_bytes=64, offset=64),
+        ]
+        hq = [keep.tile([P, CHUNK], U32, name="hq%d" % c, align_bytes=64) for c in range(CHUNKS)]
+        hs = [after_scales.tile([P, CHUNK], U8, name="hs%d" % c, align_bytes=64, offset=1088 + c * CHUNK) for c in range(CHUNKS - 1)]
+        hs.append(keep.tile([P, CHUNK], U8, name="hs3", align_bytes=64))
+        gate = [keep.tile([P, PACK, 2 * CHUNK], F32, name="gate%d" % u, align_bytes=DMA_ALIGN) for u in range(2)]
+        out32 = [keep.tile([P, PACK, 2 * CHUNK], F32, name="out32_%d" % u, align_bytes=DMA_ALIGN) for u in range(2)]
+        out_bf = [keep.tile([P, CHUNK, PACK], BF16, name="out_bf%d" % c, align_bytes=64) for c in range(CHUNKS)]
+        oq = keep.tile([P, S], U32, name="oq", align_bytes=DMA_ALIGN)
+        os_ = keep.tile([P, S], U8, name="os_", align_bytes=DMA_ALIGN)
+        out_rows = out_0.rearrange("(p t) n -> p t n", t=PACK)
+        out_words = out_1[0].rearrange("p c r -> p (c r)").bitcast(I32)
+        z = {}
 
         def within(c):
             return slice((c % 2) * CHUNK, (c % 2 + 1) * CHUNK)
 
-        def second(c):
-            for lo, hi in halves if c == 0 else ((0, PACK),):
-                bank = psum.tile([P, hi - lo, CHUNK], F32, name="zb%d_%d" % (c, lo), tag="zb%d_%d" % (c % 3, lo))
+        def round_h(copy, c, lo, hi):
+            copy(out=h_bf[c][:, lo:hi], in_=h_bank[c][:].rearrange("p t n -> p n t")[:, lo:hi])
+
+        def quant_h(c):
+            nc.vector.quantize_mx(out=hq[c][:].bitcast(FP8X4), scales=hs[c][:], in_=h_bf[c][:].rearrange("p n t -> p (n t)"))
+            for lo, hi in SLICE_PAIRS:
+                step = GATE_ORDER.index((c, lo))
+                z[c, lo] = psum.tile([P, 2, CHUNK], F32, name="z%d" % step, tag="z%d" % (step % GATE_BANKS))
                 for t in range(lo, hi):
-                    nc.tensor.matmul_mx(out=bank[:, t - lo, :], lhsT=w2w[:, 2 * t * P : 2 * (t + 1) * P].bitcast(FP4X4), lhsT_scale=w2s[:, t * P : (t + 1) * P],
+                    nc.tensor.matmul_mx(out=z[c, lo][:, t - lo, :], lhsT=w2w[:, 2 * t * P : 2 * (t + 1) * P].bitcast(FP4X4), lhsT_scale=w2s[:, t * P : (t + 1) * P],
                                         rhs=hq[c][:].bitcast(FP8X4), rhs_scale=hs[c][:], start=True, stop=True)
-                for a, b in halves:
-                    if lo <= a and b <= hi:
-                        zb[c, a] = bank[:, a - lo : b - lo, :]
 
-        def gate_and_product(pair):
-            g[pair] = keep.tile([P, PACK, 2 * CHUNK], F32, name="g%d" % pair, align_bytes=DMA_ALIGN)
-            o32[pair] = keep.tile([P, PACK, 2 * CHUNK], F32, name="o32_%d" % pair, align_bytes=DMA_ALIGN)
-            both = (2 * pair, 2 * pair + 1)
-            steps = [(c, h) for c in both for h in halves] if pair == 0 else [(c, h) for h in halves for c in both]
-            for c, (lo, hi) in steps:
-                nc.scalar.activation(out=g[pair][:, lo:hi, within(c)], in_=zb[c, lo], func=SIGMOID)
-                nc.vector.tensor_tensor(out=o32[pair][:, lo:hi, within(c)], in0=hb[c][:, lo:hi, :], in1=g[pair][:, lo:hi, within(c)], op=MULT)
-                if c == 0:
-                    nc.sync.dma_start(out=out_rows[:, lo:hi, cols(c)], in_=o32[pair][:, lo:hi, within(c)])
-                if c == 1 and hi == PACK:
-                    nc.sync.dma_start(out=out_rows[:, :, cols(c)], in_=o32[pair][:, :, within(c)])
-                if pair == 1 and c % 2 == 1:
-                    nc.sync.dma_start(out=out_rows[:, lo:hi, pair * 2 * CHUNK : (pair + 1) * 2 * CHUNK], in_=o32[pair][:, lo:hi, :])
+        def gated(c, lo, hi):
+            nc.scalar.activation(out=gate[c // 2][:, lo:hi, within(c)], in_=z[c, lo][:], func=SIGMOID)
+            nc.vector.tensor_tensor(out=out32[c // 2][:, lo:hi, within(c)], in0=h_bank[c][:, lo:hi, :], in1=gate[c // 2][:, lo:hi, within(c)], op=MULT)
 
-        def round_o(c):
-            o_bf[c] = keep.tile([P, CHUNK, PACK], BF16, name="o_bf%d" % c, align_bytes=64)
-            dst = o_bf[c][:].rearrange("p (n i) t -> p n t i", i=4)
-            src = o32[c // 2][:, :, within(c)].rearrange("p t (n i) -> p n t i", i=4)
-            if c % 2 == 0:
-                nc.scalar.copy(out=dst, in_=src)
-            else:
-                nc.vector.tensor_copy(out=dst, in_=src)
+        def round_out(copy, c):
+            copy(out=out_bf[c][:].rearrange("p (n i) t -> p n t i", i=4), in_=out32[c // 2][:, :, within(c)].rearrange("p t (n i) -> p n t i", i=4))
 
-        def quant_o(c):
-            nc.vector.quantize_mx(out=oq[:, cols(c)].bitcast(FP8X4), scales=os_[:, cols(c)], in_=o_bf[c][:].rearrange("p n t -> p (n t)"))
+        def quant_out(c):
+            nc.vector.quantize_mx(out=oq[:, cols(c)].bitcast(FP8X4), scales=os_[:, cols(c)], in_=out_bf[c][:].rearrange("p n t -> p (n t)"))
             if c % 2 == 1:
                 both = slice((c - 1) * CHUNK, (c + 1) * CHUNK)
                 nc.scalar.dma_start(out=out_words[:, both], in_=oq[:, both].bitcast(I32))
 
-        quant_w1(0)
-        quant_w1(1)
-        gather(0)
-        first(0)
-        for c in range(1, CHUNKS):
-            if c == CHUNKS - 1:
-                deal_scales()
-            gather(c)
-            first(c)
+        for c in range(CHUNKS - 1):
+            round_h(nc.scalar.copy, c, 0, CHUNK)
+        quant_h(0)
+        round_h(nc.vector.tensor_copy, 3, 0, HALF)
+        quant_h(1)
+        round_h(nc.vector.tensor_copy, 3, HALF, CHUNK)
+        quant_h(2)
+        quant_h(3)
+        for lo, hi in SLICE_PAIRS:
+            gated(0, lo, hi)
+            nc.sync.dma_start(out=out_rows[:, lo:hi, cols(0)], in_=out32[0][:, lo:hi, within(0)])
+        for lo, hi in SLICE_PAIRS:
+            gated(1, lo, hi)
+        nc.sync.dma_start(out=out_rows[:, :, cols(1)], in_=out32[0][:, :, within(1)])
+        for lo, hi in SLICE_PAIRS:
+            gated(2, lo, hi)
+            gated(3, lo, hi)
+            nc.sync.dma_start(out=out_rows[:, lo:hi, 2 * CHUNK : S], in_=out32[1][:, lo:hi, :])
         for c in range(CHUNKS):
-            round_h(c)
+            round_out(nc.scalar.copy if c % 2 == 0 else nc.vector.tensor_copy, c)
         for c in range(CHUNKS):
-            quant_h(c)
-            second(c)
-            if c < 2:
-                round_last(c)
-        for pair in range(CHUNKS // 2):
-            gate_and_product(pair)
-        for c in range(CHUNKS):
-            round_o(c)
-        for c in range(CHUNKS):
-            quant_o(c)
+            quant_out(c)
         scale_rows = out_2[0].bitcast(I32)
         for q in range(4):
             eng = nc.sync if q < 3 else nc.scalar

@@ -20,8 +20,9 @@ CHUNK = 128
 CHUNKS = S // CHUNK
 HALF = CHUNK // 2
 W1_FIRST = 192
-FIRST_CAST_VECTOR = 18
-CAST_VECTOR = (52, 44)
+FIRST_CAST_VECTOR = 24
+WARM_VECTOR = 384
+CAST_VECTOR = (48, 42)
 WARM_M = 32
 WARM_N = 512
 WARM_PASSES = 3
@@ -82,8 +83,10 @@ def tile_picked_zgrn_lin_po_kernel(tc, x_words, x_scales, w1, w2_words, w2_scale
         wide_q = keep.tile([P, WARM_N], U32, name="wide_q", align_bytes=64)
         wide_s = keep.tile([P, WARM_N], U8, name="wide_s", align_bytes=64)
         reps = WARM_N // WARM_M
-        nc.scalar.copy(out=wide_q[:].rearrange("p (r m) -> p r m", r=reps), in_=warm_q[:].unsqueeze(1).to_broadcast([P, reps, WARM_M]))
         nc.scalar.copy(out=wide_s[:].bitcast(U32).rearrange("p (r m) -> p r m", r=reps), in_=warm_s[:].bitcast(U32).unsqueeze(1).to_broadcast([P, reps, WARM_M // 4]))
+        for copy, lo, hi in ((nc.vector.tensor_copy, 0, WARM_VECTOR), (nc.scalar.copy, WARM_VECTOR, WARM_N)):
+            reps = (hi - lo) // WARM_M
+            copy(out=wide_q[:, lo:hi].rearrange("p (r m) -> p r m", r=reps), in_=warm_q[:].unsqueeze(1).to_broadcast([P, reps, WARM_M]))
         warm_bank = psum.tile([WARM_M, WARM_N], F32, name="warm_bank", tag="z3")
         for n_pass in range(WARM_PASSES):
             nc.tensor.matmul_mx(out=warm_bank[:], lhsT=warm_q[:].bitcast(FP8X4), lhsT_scale=warm_s[:],

@@ -60,12 +60,12 @@ def tile_picked_zgrn_lin_po_kernel(tc, x_words, x_scales, w1, w2_words, w2_scale
         nc.sync.dma_start(out=w1_a[:], in_=w1_rows[:, :, 0:W1_FIRST])
         nc.sync.dma_start(offsets[:], offs)
         for q in range(4):
-            nc.sync.dma_start(out=xs_win[32 * q : 32 * q + 4, :].bitcast(I32), in_=x_scales[0, 4 * q : 4 * q + 4, :].bitcast(I32))
+            nc.sync.dma_start(out=xs_win[q:P:32, :].bitcast(I32), in_=x_scales[0, q:16:4, :].bitcast(I32))
         nc.sync.dma_start(out=w1_b[:], in_=w1_rows[:, :, W1_FIRST:H])
         nc.sync.dma_start(out=xw_win[:], in_=x_words[0].rearrange("p c r -> p (c r)").bitcast(I32))
         nc.sync.dma_start(out=w2w_raw[:].bitcast(I32), in_=w2_words[0].bitcast(I32))
         for q in range(4):
-            nc.sync.dma_start(out=w2s_raw[32 * q : 32 * q + 4, :].bitcast(I32), in_=w2_scales[0, 4 * q : 4 * q + 4, :].bitcast(I32))
+            nc.sync.dma_start(out=w2s_raw[q:P:32, :].bitcast(I32), in_=w2_scales[0, q:16:4, :].bitcast(I32))
 
         w1_bf = keep.tile([P, H * PACK], BF16, name="w1_bf", align_bytes=64)
         w1_dealt = w1_bf[:].rearrange("p (t m j) -> p m j t", t=PACK, j=PACK)
@@ -193,4 +193,4 @@ def tile_picked_zgrn_lin_po_kernel(tc, x_words, x_scales, w1, w2_words, w2_scale
         scale_rows = out_2[0].bitcast(I32)
         for q in range(4):
             eng = nc.sync if q < 3 else nc.scalar
-            eng.dma_start(out=scale_rows[4 * q : 4 * q + 4, :], in_=os_[32 * q : 32 * q + 4, :].bitcast(I32))
+            eng.dma_start(out=scale_rows[q:16:4, :], in_=os_[q:P:32, :].bitcast(I32))

@@ -19,10 +19,10 @@ K, T, S, H = 512, 1024, 512, 512
 CHUNK = 128
 CHUNKS = S // CHUNK
 HALF = CHUNK // 2
-W1_FIRST = 192
-FIRST_CAST_VECTOR = 24
+W1_FIRST = 128
+FIRST_CAST_VECTOR = 18
 WARM_VECTOR = 384
-CAST_VECTOR = (48, 42)
+CAST_VECTOR = (62, 58)
 WARM_M = 32
 WARM_N = 512
 WARM_PASSES = 3

@@ -192,5 +192,5 @@ def tile_picked_zgrn_lin_po_kernel(tc, x_words, x_scales, w1, w2_words, w2_scale
             quant_out(c)
         scale_rows = out_2[0].bitcast(I32)
         for q in range(4):
-            eng = nc.sync if q < 3 else nc.scalar
+            eng = nc.sync if q < 2 else nc.scalar
             eng.dma_start(out=scale_rows[q:16:4, :], in_=os_[q:P:32, :].bitcast(I32))

from contextlib import ExitStack

import concourse.mybir as mybir

F32 = mybir.dt.float32
BF16 = mybir.dt.bfloat16
I32 = mybir.dt.int32
U32 = mybir.dt.uint32
U16 = mybir.dt.uint16
U8 = mybir.dt.uint8
FP8X4 = mybir.dt.float8_e4m3fn_x4
FP4X4 = mybir.dt.float4_e2m1fn_x4
SIGMOID = mybir.ActivationFunctionType.Sigmoid
MULT = mybir.AluOpType.mult

P = 128
PACK = 4
K, T, S, H = 512, 1024, 512, 512
CHUNK = 128
CHUNKS = S // CHUNK
HALF = CHUNK // 2
W1_FIRST = 128
FIRST_CAST_VECTOR = 18
WARM_VECTOR = 384
CAST_VECTOR = (62, 58)
WARM_M = 32
WARM_N = 512
WARM_PASSES = 3
DMA_ALIGN = 256
FLOPS = 2 * K * H * S + 2 * H * H * S
SLICE_PAIRS = ((0, 2), (2, 4))
GATE_ORDER = ((0, 0), (0, 2), (1, 0), (1, 2), (2, 0), (3, 0), (2, 2), (3, 2))
GATE_BANKS = 4


def tile_picked_zgrn_lin_po_kernel(tc, x_words, x_scales, w1, w2_words, w2_scales, offs, out_0, out_1, out_2):
    nc = tc.nc
    with ExitStack() as ctx:
        keep = ctx.enter_context(tc.tile_pool(name="keep", bufs=1))
        after_words = ctx.enter_context(tc.tile_pool(name="after_words", bufs=1))
        after_scales = ctx.enter_context(tc.tile_pool(name="after_scales", bufs=1))
        psum = ctx.enter_context(tc.psum_pool(name="psum", bufs=1))

        xs_win = keep.tile([P, T], U8, name="xs_win", align_bytes=DMA_ALIGN)
        nc.vector.memset(xs_win[:].bitcast(I32), 0)
        table_in = keep.tile([P, 8], F32, name="table_in")
        table_out = keep.tile([P, 8], F32, name="table_out")
        nc.vector.memset(table_in[:], 0.0)
        nc.scalar.activation(out=table_out[:], in_=table_in[:], func=SIGMOID)

        offsets = keep.tile([P, S // 16], U16, name="offsets", align_bytes=DMA_ALIGN)
        w1_rows = w1.rearrange("(p j) c -> p j c", j=PACK)
        w1_a = keep.tile([P, PACK, W1_FIRST], F32, name="w1_a", align_bytes=DMA_ALIGN)
        w1_b = keep.tile([P, PACK, H - W1_FIRST], F32, name="w1_b", align_bytes=DMA_ALIGN)
        xw_win = keep.tile([P, T], I32, name="xw_win", align_bytes=DMA_ALIGN)
        w2w_raw = after_words.tile([P, 2 * H], U8, name="w2w_raw", align_bytes=DMA_ALIGN, offset=1024)
        w2s_raw = after_scales.tile([P, H], U8, name="w2s_raw", align_bytes=DMA_ALIGN, offset=1024)
        nc.vector.memset(w2s_raw[:].bitcast(I32), 0)

        nc.sync.dma_start(out=w1_a[:], in_=w1_rows[:, :, 0:W1_FIRST])
        nc.sync.dma_start(offsets[:], offs)
        for q in range(4):
            nc.sync.dma_start(out=xs_win[q:P:32, :].bitcast(I32), in_=x_scales[0, q:16:4, :].bitcast(I32))
        nc.sync.dma_start(out=w1_b[:], in_=w1_rows[:, :, W1_FIRST:H])
        nc.sync.dma_start(out=xw_win[:], in_=x_words[0].rearrange("p c r -> p (c r)").bitcast(I32))
        nc.sync.dma_start(out=w2w_raw[:].bitcast(I32), in_=w2_words[0].bitcast(I32))
        for q in range(4):
            nc.sync.dma_start(out=w2s_raw[q:P:32, :].bitcast(I32), in_=w2_scales[0, q:16:4, :].bitcast(I32))

        w1_bf = keep.tile([P, H * PACK], BF16, name="w1_bf", align_bytes=64)
        w1_dealt = w1_bf[:].rearrange("p (t m j) -> p m j t", t=PACK, j=PACK)
        src_a = w1_a[:].rearrange("p j (m t) -> p m j t", t=PACK)
        src_b = w1_b[:].rearrange("p j (m t) -> p m j t", t=PACK)
        rest = w1_dealt[:, W1_FIRST // PACK : P]
        warm_bf = keep.tile([P, WARM_M * PACK], BF16, name="warm_bf", align_bytes=64)
        nc.vector.tensor_copy(out=warm_bf[:], in_=w1_a[:, 0, 0 : WARM_M * PACK])
        nc.vector.tensor_copy(out=w1_dealt[:, 0:FIRST_CAST_VECTOR], in_=src_a[:, 0:FIRST_CAST_VECTOR])
        nc.scalar.copy(out=w1_dealt[:, FIRST_CAST_VECTOR : W1_FIRST // PACK], in_=src_a[:, FIRST_CAST_VECTOR:])
        warm_q = keep.tile([P, WARM_M], U32, name="warm_q", align_bytes=64)
        warm_s = keep.tile([P, WARM_M], U8, name="warm_s", align_bytes=64)
        nc.vector.memset(warm_s[:].bitcast(I32), 0)
        nc.vector.quantize_mx(out=warm_q[:].bitcast(FP8X4), scales=warm_s[:], in_=warm_bf[:])
        wide_q = keep.tile([P, WARM_N], U32, name="wide_q", align_bytes=64)
        wide_s = keep.tile([P, WARM_N], U8, name="wide_s", align_bytes=64)
        reps = WARM_N // WARM_M
        nc.scalar.copy(out=wide_s[:].bitcast(U32).rearrange("p (r m) -> p r m", r=reps), in_=warm_s[:].bitcast(U32).unsqueeze(1).to_broadcast([P, reps, WARM_M // 4]))
        for copy, lo, hi in ((nc.vector.tensor_copy, 0, WARM_VECTOR), (nc.scalar.copy, WARM_VECTOR, WARM_N)):
            reps = (hi - lo) // WARM_M
            copy(out=wide_q[:, lo:hi].rearrange("p (r m) -> p r m", r=reps), in_=warm_q[:].unsqueeze(1).to_broadcast([P, reps, WARM_M]))
        warm_bank = psum.tile([WARM_M, WARM_N], F32, name="warm_bank", tag="z3")
        for n_pass in range(WARM_PASSES):
            nc.tensor.matmul_mx(out=warm_bank[:], lhsT=warm_q[:].bitcast(FP8X4), lhsT_scale=warm_s[:],
                                rhs=wide_q[:].bitcast(FP8X4), rhs_scale=wide_s[:], start=True, stop=True)
        xs = keep.tile([P, S], U8, name="xs", align_bytes=64)
        nc.vector.tensor_copy(xs[:], xs_win[:].indirect(offsets[:]))
        for (lo, hi), cut in zip(SLICE_PAIRS, CAST_VECTOR):
            nc.vector.tensor_copy(out=rest[:, 0:cut, :, lo:hi], in_=src_b[:, 0:cut, :, lo:hi])
            nc.scalar.copy(out=rest[:, cut:, :, lo:hi], in_=src_b[:, cut:, :, lo:hi])
        w1q = keep.tile([P, H], U32, name="w1q", align_bytes=64)
        w1s = keep.tile([P, H], U8, name="w1s", align_bytes=64)
        for lo, hi in SLICE_PAIRS:
            nc.vector.quantize_mx(out=w1q[:, lo * P : hi * P].bitcast(FP8X4), scales=w1s[:, lo * P : hi * P], in_=w1_bf[:, lo * P * PACK : hi * P * PACK])

        def cols(c):
            return slice(c * CHUNK, (c + 1) * CHUNK)

        h_bank = []
        for c in range(CHUNKS):
            if c == CHUNKS - 1:
                xw = after_words.tile([P, CHUNK], U32, name="xw%d" % c, align_bytes=64, offset=2560)
            else:
                xw = keep.tile([P, CHUNK], U32, name="xw%d" % c, align_bytes=64)
            nc.vector.tensor_copy(xw[:], xw_win[:].bitcast(U32).indirect(offsets[:, c * 8 : (c + 1) * 8]))
            bank = psum.tile([P, PACK, CHUNK], F32, name="h_bank%d" % c)
            for t in range(PACK):
                nc.tensor.matmul_mx(out=bank[:, t, :], lhsT=w1q[:, t * P : (t + 1) * P].bitcast(FP8X4), lhsT_scale=w1s[:, t * P : (t + 1) * P],
                                    rhs=xw[:].bitcast(FP8X4), rhs_scale=xs[:, cols(c)], start=True, stop=True)
            h_bank.append(bank)

        w2w = keep.tile([P, 2 * H], U8, name="w2w", align_bytes=64)
        w2s = keep.tile([P, H], U8, name="w2s", align_bytes=64)
        nc.scalar.copy(out=w2w[:].bitcast(U16).rearrange("p (t m) -> p t m", t=PACK), in_=w2w_raw[:].bitcast(U16).rearrange("p (m t) -> p t m", t=PACK))
        nc.vector.tensor_copy(out=w2s[:].rearrange("p (t m) -> p t m", t=PACK), in_=w2s_raw[:].rearrange("p (m t) -> p t m", t=PACK))

        h_bf = [
            after_words.tile([P, CHUNK, PACK], BF16, name="h_bf0", align_bytes=64, offset=512),
            after_words.tile([P, CHUNK, PACK], BF16, name="h_bf1", align_bytes=64, offset=1536),
            after_words.tile([P, CHUNK, PACK], BF16, name="h_bf2", align_bytes=64, offset=2560),
            after_scales.tile([P, CHUNK, PACK], BF16, name="h_bf3", align_bytes=64, offset=64),
        ]
        hq = [keep.tile([P, CHUNK], U32, name="hq%d" % c, align_bytes=64) for c in range(CHUNKS)]
        hs = [after_scales.tile([P, CHUNK], U8, name="hs%d" % c, align_bytes=64, offset=1088 + c * CHUNK) for c in range(CHUNKS - 1)]
        hs.append(keep.tile([P, CHUNK], U8, name="hs3", align_bytes=64))
        gate = [keep.tile([P, PACK, 2 * CHUNK], F32, name="gate%d" % u, align_bytes=DMA_ALIGN) for u in range(2)]
        out32 = [keep.tile([P, PACK, 2 * CHUNK], F32, name="out32_%d" % u, align_bytes=DMA_ALIGN) for u in range(2)]
        out_bf = [keep.tile([P, CHUNK, PACK], BF16, name="out_bf%d" % c, align_bytes=64) for c in range(CHUNKS)]
        oq = keep.tile([P, S], U32, name="oq", align_bytes=DMA_ALIGN)
        os_ = keep.tile([P, S], U8, name="os_", align_bytes=DMA_ALIGN)
        out_rows = out_0.rearrange("(p t) n -> p t n", t=PACK)
        out_words = out_1[0].rearrange("p c r -> p (c r)").bitcast(I32)
        z = {}

        def within(c):
            return slice((c % 2) * CHUNK, (c % 2 + 1) * CHUNK)

        def round_h(copy, c, lo, hi):
            copy(out=h_bf[c][:, lo:hi], in_=h_bank[c][:].rearrange("p t n -> p n t")[:, lo:hi])

        def quant_h(c):
            nc.vector.quantize_mx(out=hq[c][:].bitcast(FP8X4), scales=hs[c][:], in_=h_bf[c][:].rearrange("p n t -> p (n t)"))
            for lo, hi in SLICE_PAIRS:
                step = GATE_ORDER.index((c, lo))
                z[c, lo] = psum.tile([P, 2, CHUNK], F32, name="z%d" % step, tag="z%d" % (step % GATE_BANKS))
                for t in range(lo, hi):
                    nc.tensor.matmul_mx(out=z[c, lo][:, t - lo, :], lhsT=w2w[:, 2 * t * P : 2 * (t + 1) * P].bitcast(FP4X4), lhsT_scale=w2s[:, t * P : (t + 1) * P],
                                        rhs=hq[c][:].bitcast(FP8X4), rhs_scale=hs[c][:], start=True, stop=True)

        def gated(c, lo, hi):
            nc.scalar.activation(out=gate[c // 2][:, lo:hi, within(c)], in_=z[c, lo][:], func=SIGMOID)
            nc.vector.tensor_tensor(out=out32[c // 2][:, lo:hi, within(c)], in0=h_bank[c][:, lo:hi, :], in1=gate[c // 2][:, lo:hi, within(c)], op=MULT)

        def round_out(copy, c):
            copy(out=out_bf[c][:].rearrange("p (n i) t -> p n t i", i=4), in_=out32[c // 2][:, :, within(c)].rearrange("p t (n i) -> p n t i", i=4))

        def quant_out(c):
            nc.vector.quantize_mx(out=oq[:, cols(c)].bitcast(FP8X4), scales=os_[:, cols(c)], in_=out_bf[c][:].rearrange("p n t -> p (n t)"))
            if c % 2 == 1:
                both = slice((c - 1) * CHUNK, (c + 1) * CHUNK)
                nc.scalar.dma_start(out=out_words[:, both], in_=oq[:, both].bitcast(I32))

        for c in range(CHUNKS - 1):
            round_h(nc.scalar.copy, c, 0, CHUNK)
        quant_h(0)
        round_h(nc.vector.tensor_copy, 3, 0, HALF)
        quant_h(1)
        round_h(nc.vector.tensor_copy, 3, HALF, CHUNK)
        quant_h(2)
        quant_h(3)
        for lo, hi in SLICE_PAIRS:
            gated(0, lo, hi)
            nc.sync.dma_start(out=out_rows[:, lo:hi, cols(0)], in_=out32[0][:, lo:hi, within(0)])
        for lo, hi in SLICE_PAIRS:
            gated(1, lo, hi)
        nc.sync.dma_start(out=out_rows[:, :, cols(1)], in_=out32[0][:, :, within(1)])
        for lo, hi in SLICE_PAIRS:
            gated(2, lo, hi)
            gated(3, lo, hi)
            nc.sync.dma_start(out=out_rows[:, lo:hi, 2 * CHUNK : S], in_=out32[1][:, lo:hi, :])
        for c in range(CHUNKS):
            round_out(nc.scalar.copy if c % 2 == 0 else nc.vector.tensor_copy, c)
        for c in range(CHUNKS):
            quant_out(c)
        scale_rows = out_2[0].bitcast(I32)
        for q in range(4):
            eng = nc.sync if q < 2 else nc.scalar
            eng.dma_start(out=scale_rows[q:16:4, :], in_=os_[q:P:32, :].bitcast(I32))
